import numpy as np
import ml_dtypes


def mxq(x, axis, fmt="e4m3"):
    dtype, down = {"e4m3": (ml_dtypes.float8_e4m3fn, 7), "e5m2": (ml_dtypes.float8_e5m2, 14)}[fmt]
    v = np.moveaxis(np.asarray(x, np.float32).astype(ml_dtypes.bfloat16).astype(np.float64), axis, -1)
    blocks = v.reshape(v.shape[:-1] + (-1, 32))
    amax = np.abs(blocks).max(-1, keepdims=True)
    byte = np.maximum(np.where(amax > 0, np.frexp(amax)[1] - 1 + 127, 0) - down, 1)
    scale = np.exp2(byte - 127.0)
    codes = (blocks / scale).astype(np.float32).astype(dtype).astype(np.float64)
    return np.moveaxis((codes * scale).reshape(v.shape), -1, axis)


WIDE = False


def mx_kscale(k):
    if not WIDE:
        return np.ones(k)
    levels = np.array([10, -10, 5, -5, 0])
    if k % 512:
        return np.exp2(np.random.permutation(np.resize(levels, k // 32))).repeat(32)
    a = np.empty((k // 512, 16))
    for p in range(k // 512):
        a[p, :8] = np.random.permutation(np.resize(levels, 8))
        for g in range(8):
            far = levels[np.abs(levels - a[p, g]) >= 10]
            a[p, g + 8] = far[np.random.randint(len(far))]
    return np.exp2(a.ravel()).repeat(32)


def f64(x):
    return np.asarray(x).astype(np.float64)


def striped(idx):
    return np.tile(idx.reshape(-1, 16).T, (8, 1)).astype(np.uint16)


def unstriped(offs):
    return offs[:16].T.reshape(-1).astype(np.int64)


def silu(v):
    return v / (1.0 + np.exp(-np.maximum(v, -700.0)))


K, T, S, V, N = 1024, 2048, 1024, 512, 128


def setup_inputs():
    n = np.random.standard_normal
    s = mx_kscale(K)[:, None]
    return {
        "xT": (n((K, T)) * s).astype(np.float32),
        "w1": (n((K, N)) / np.sqrt(K) / s).astype(np.float32),
        "w2": (n((K, N)) / np.sqrt(K) / s).astype(np.float32),
        "w3": (n((K, N)) / np.sqrt(K) / s).astype(np.float32),
        "offs": striped(np.random.permutation(T)[:S]),
        "cen": striped(np.random.permutation(S)[:V]),
        "pos1": striped(np.random.permutation(S)[:V]),
        "pos2": striped(np.random.permutation(S)[:V]),
    }


def reference(xT, w1, w2, w3, offs, cen, pos1, pos2):
    xq = mxq(f64(xT)[:, unstriped(offs)], 0, "e4m3")
    h = mxq(f64(w3), 0, "e4m3").T @ xq
    g = mxq(f64(w1), 0, "e4m3").T @ xq
    gc = g[:, unstriped(cen)]
    s = mxq(f64(w2), 0, "e4m3").T @ xq
    sc = s[:, unstriped(cen)]
    return silu(h[:, unstriped(pos1)] * gc + sc) + silu(h[:, unstriped(pos2)] * gc + sc)

@@ -1,0 +1,182 @@
+from contextlib import ExitStack
+
+import concourse.mybir as mybir
+from concourse.masks import make_identity
+
+K, T, S, V, N = 1024, 2048, 1024, 512, 128
+FLOPS = 3 * 2 * K * S * N
+
+F32 = mybir.dt.float32
+BF16 = mybir.dt.bfloat16
+I32 = mybir.dt.int32
+U32 = mybir.dt.uint32
+U16 = mybir.dt.uint16
+U8 = mybir.dt.uint8
+FP8X4 = mybir.dt.float8_e4m3fn_x4
+MULT = mybir.AluOpType.mult
+ADD = mybir.AluOpType.add
+SILU = mybir.ActivationFunctionType.Silu
+
+P = 128
+HALF = 512
+CHUNKS = [[(1024, 384), (1024, 384)], [(1024, 1024), (1024, 384)], [(1024, 1024), (1024, 576)], [(1024, 1024), (512, 0), (256, 0), (256, 256)]]
+TAIL = "v"
+PIECES = [192, 192, 128]
+
+
+def tile_picked_filmg_silu_e_kernel(tc, xT, w1, w2, w3, offs, cen, pos1, pos2, out):
+    nc = tc.nc
+    with ExitStack() as ctx:
+        lists = ctx.enter_context(tc.tile_pool(name="lists", bufs=1))
+        sb = ctx.enter_context(tc.tile_pool(name="sb", bufs=1))
+        ps = ctx.enter_context(tc.psum_pool(name="ps", bufs=1))
+
+        offs_sb = lists.tile([P, S // 16], U16, name="offs_sb")
+        cen_sb = lists.tile([P, V // 16], U16, name="cen_sb")
+        pos_sb = [lists.tile([P, V // 16], U16, name="pos%d_sb" % d) for d in range(2)]
+
+        warm_in = sb.tile([P, 8], F32, name="warm_in")
+        warm_out = sb.tile([P, 8], F32, name="warm_out")
+        nc.gpsimd.memset(warm_in[:], 0.0)
+        nc.scalar.activation(warm_out[:], warm_in[:], SILU)
+        if TAIL == "pe":
+            ident = sb.tile([P, P], F32, name="ident")
+            make_identity(nc, ident[:])
+
+        x_rows = xT.rearrange("(z p u e) t -> z u p e t", z=2, p=P, u=2, e=2)
+        picked = [sb.tile([P, 2, 2, HALF], U32, name="picked%d" % z, tag="picked%d" % z, align_bytes=64) for z in range(2)]
+        x_codes = [sb.tile([P, S], U32, name="xc%d" % z, align_bytes=64) for z in range(2)]
+        x_scales = [sb.tile([P, S], U8, name="xs%d" % z, align_bytes=64) for z in range(2)]
+
+        def load_pair(z, u):
+            window = sb.tile([P, T, 2], BF16, name="window%d%d" % (z, u))
+            c0 = 0
+            for i, (width, on_scalar) in enumerate(CHUNKS[2 * z + u]):
+                raw = sb.tile([P, 2, width], F32, name="raw%d%d%d" % (z, u, i))
+                nc.sync.dma_start(raw[:], x_rows[z, u, :, :, c0 : c0 + width])
+                if (z, u, i) == (0, 0, 0):
+                    nc.sync.dma_start(offs_sb[:], offs)
+                if (z, u, i) == (1, 0, 0):
+                    nc.sync.dma_start(cen_sb[:], cen)
+                    nc.sync.dma_start(pos_sb[0][:], pos1)
+                    nc.sync.dma_start(pos_sb[1][:], pos2)
+                src = raw[:].rearrange("p e t -> p t e")
+                if on_scalar > 0:
+                    nc.scalar.copy(window[:, c0 : c0 + on_scalar, :], src[:, 0:on_scalar, :])
+                if on_scalar < width:
+                    nc.vector.tensor_copy(window[:, c0 + on_scalar : c0 + width, :], src[:, on_scalar:width, :])
+                c0 += width
+            words = window[:].rearrange("p t e -> p (t e)").bitcast(U32)
+            if u == 1:
+                for a in range(2):
+                    nc.vector.tensor_copy(picked[z][:, a, u, :], words.indirect(offs_sb[:, 32 * a : 32 * (a + 1)]))
+            else:
+                nc.vector.tensor_copy(picked[z][:, :, u, :], words.indirect(offs_sb[:]))
+
+        def weave(z, a0, a1, on_scalar, tag):
+            grouped = sb.tile([P, 4 * HALF * (a1 - a0)], BF16, name="grouped%d%d" % (z, a0), tag=tag, align_bytes=64)
+            dt = U32 if on_scalar else I32
+            dst = grouped[:].bitcast(dt).rearrange("p (a n u) -> p a n u", n=HALF, u=2)
+            src = picked[z][:, a0:a1, :, :].bitcast(dt).rearrange("p a u n -> p a n u")
+            if on_scalar:
+                nc.scalar.copy(dst, src)
+            else:
+                nc.vector.tensor_copy(dst, src)
+            return grouped
+
+        def quantize_x(z, a, grouped, n0, n1):
+            cols = slice(a * HALF + n0, a * HALF + n1)
+            nc.vector.quantize_mx(out=x_codes[z][:, cols].bitcast(FP8X4), scales=x_scales[z][:, cols], in_=grouped[:, 4 * n0 : 4 * n1])
+
+        def load_w(name, w):
+            raw = sb.tile([P, 2, 4, N], F32, name="raw_" + name, tag="raw_" + name, align_bytes=64)
+            nc.sync.dma_start(raw[:], w.rearrange("(z p j) n -> p z j n", z=2, p=P, j=4))
+            return raw
+
+        def cast_w(name, raw, on_scalar, tag):
+            grouped = sb.tile([P, 2, N, 4], BF16, name="grouped_" + name, tag=tag, align_bytes=64)
+            dst = grouped[:].rearrange("p z (c i) j -> p z c j i", i=4)
+            src = raw[:].rearrange("p z j (c i) -> p z c j i", i=4)
+            if on_scalar:
+                nc.scalar.copy(dst, src)
+            else:
+                nc.vector.tensor_copy(dst, src)
+            return grouped
+
+        def quantize_w(name, grouped, tag):
+            codes = sb.tile([P, 2 * N], U32, name="codes_" + name, tag=tag, align_bytes=64)
+            scales = sb.tile([P, 2 * N], U8, name="scales_" + name, align_bytes=64)
+            nc.vector.quantize_mx(out=codes[:].bitcast(FP8X4), scales=scales[:], in_=grouped[:].rearrange("p z n j -> p (z n j)"))
+            return codes, scales
+
+        def product(name, wq, parts, tag):
+            codes, scales = wq
+            res = sb.tile([P, S], F32, name="res_" + name, tag=tag, align_bytes=64)
+            acc = [ps.tile([P, c1 - c0], F32, name="acc_%s%d" % (name, c0)) for c0, c1, on_scalar in parts]
+            for z in range(2):
+                for bank, (c0, c1, on_scalar) in zip(acc, parts):
+                    nc.tensor.matmul_mx(
+                        out=bank[:],
+                        lhsT=codes[:, z * N : (z + 1) * N].bitcast(FP8X4),
+                        lhsT_scale=scales[:, z * N : (z + 1) * N],
+                        rhs=x_codes[z][:, c0:c1].bitcast(FP8X4),
+                        rhs_scale=x_scales[z][:, c0:c1],
+                        start=(z == 0),
+                        stop=(z == 1),
+                    )
+            for bank, (c0, c1, on_scalar) in zip(acc, parts):
+                if on_scalar:
+                    nc.scalar.copy(res[:, c0:c1], bank[:])
+                else:
+                    nc.vector.tensor_copy(res[:, c0:c1], bank[:])
+            return res
+
+        load_pair(0, 0)
+        load_pair(0, 1)
+        gx = [weave(0, a, a + 1, False, "gx0%d" % a) for a in range(2)]
+        for a in range(2):
+            quantize_x(0, a, gx[a], 0, HALF)
+        load_pair(1, 0)
+        raw1 = load_w("w1", w1)
+        g1 = cast_w("w1", raw1, True, "grouped_w1")
+        q1 = quantize_w("w1", g1, "codes_w1")
+        load_pair(1, 1)
+        raw3 = load_w("w3", w3)
+        raw2 = load_w("w2", w2)
+        g3 = cast_w("w3", raw3, True, "grouped_w3")
+        ga = weave(1, 0, 1, False, "gx10")
+        gb = weave(1, 1, 2, True, "raw_w3")
+        quantize_x(1, 0, ga, 0, HALF)
+        quantize_x(1, 1, gb, 0, HALF // 2)
+        quantize_x(1, 1, gb, HALF // 2, HALF)
+        g2 = cast_w("w2", raw2, True, "picked1")
+        g_sb = product("g", q1, [(0, 512, True), (512, 768, False), (768, 1024, False)], "raw_w2")
+        q3 = quantize_w("w3", g3, "raw_w3")
+        q2 = quantize_w("w2", g2, "codes_w2")
+        h_sb = product("h", q3, [(0, 512, True), (512, 1024, True)], "res_h")
+        s_sb = product("s", q2, [(0, 512, True), (512, 1024, True)], "res_s")
+
+        gc = sb.tile([P, V], F32, name="gc")
+        sc = sb.tile([P, V], F32, name="sc")
+        nc.vector.tensor_copy(gc[:], g_sb[:].indirect(cen_sb[:]))
+        prod = sb.tile([P, 2, V], F32, name="prod")
+        for d in range(2):
+            nc.vector.tensor_tensor(prod[:, d, :], h_sb[:].indirect(pos_sb[d][:]), gc[:], MULT)
+        nc.vector.tensor_copy(sc[:], s_sb[:].indirect(cen_sb[:]))
+        acts = []
+        v0 = 0
+        for i, width in enumerate(PIECES):
+            cols = slice(v0, v0 + width)
+            pre = sb.tile([P, 2, width], F32, name="pre%d" % i)
+            act = sb.tile([P, 2, width], F32, name="act%d" % i)
+            nc.vector.tensor_tensor(pre[:], prod[:, :, cols], sc[:, cols].unsqueeze(1).to_broadcast([P, 2, width]), ADD)
+            nc.scalar.activation(act[:], pre[:], SILU)
+            acts.append(act)
+            v0 += width
+        v0 = 0
+        for i, width in enumerate(PIECES):
+            cols = slice(v0, v0 + width)
+            res = sb.tile([P, width], F32, name="res%d" % i)
+            nc.vector.tensor_tensor(res[:], acts[i][:, 0, :], acts[i][:, 1, :], ADD)
+            nc.sync.dma_start(out[:, cols], res[:])
+            v0 += width

@@ -19,7 +19,7 @@ SILU = mybir.ActivationFunctionType.Silu
 
 P = 128
 HALF = 512
-CHUNKS = [[(1024, 384), (1024, 384)], [(1024, 1024), (1024, 384)], [(1024, 1024), (1024, 576)], [(1024, 1024), (512, 0), (256, 0), (256, 256)]]
+CHUNKS = [[(2048, 704)], [(1024, 1024), (1024, 384)], [(1024, 1024), (1024, 576)], [(1024, 1024), (512, 0), (512, 176)]]
 TAIL = "v"
 PIECES = [192, 192, 128]
 
@@ -29,6 +29,7 @@ def tile_picked_filmg_silu_e_kernel(tc, xT, w1, w2, w3, offs, cen, pos1, pos2, o
     with ExitStack() as ctx:
         lists = ctx.enter_context(tc.tile_pool(name="lists", bufs=1))
         sb = ctx.enter_context(tc.tile_pool(name="sb", bufs=1))
+        shared = ctx.enter_context(tc.tile_pool(name="shared", bufs=1))
         ps = ctx.enter_context(tc.psum_pool(name="ps", bufs=1))
 
         offs_sb = lists.tile([P, S // 16], U16, name="offs_sb")
@@ -44,8 +45,14 @@ def tile_picked_filmg_silu_e_kernel(tc, xT, w1, w2, w3, offs, cen, pos1, pos2, o
             make_identity(nc, ident[:])
 
         x_rows = xT.rearrange("(z p u e) t -> z u p e t", z=2, p=P, u=2, e=2)
-        picked = [sb.tile([P, 2, 2, HALF], U32, name="picked%d" % z, tag="picked%d" % z, align_bytes=64) for z in range(2)]
-        x_codes = [sb.tile([P, S], U32, name="xc%d" % z, align_bytes=64) for z in range(2)]
+        picked0 = sb.tile([P, 2, 2, HALF], U32, name="picked0")
+        picked1a = shared.tile([P, 2, HALF], U32, name="picked1a", offset=0, align_bytes=64)
+        picked1b = sb.tile([P, 2, HALF], U32, name="picked1b")
+        picked = [[picked0[:, 0], picked0[:, 1]], [picked1a[:], picked1b[:]]]
+        x_codes0 = sb.tile([P, S], U32, name="xc0", align_bytes=64)
+        x_codes1a = sb.tile([P, HALF], U32, name="xc1a", align_bytes=64)
+        x_codes1b = shared.tile([P, HALF], U32, name="xc1b", offset=2048, align_bytes=64)
+        x_codes = [[x_codes0[:, 0:HALF], x_codes0[:, HALF:S]], [x_codes1a[:], x_codes1b[:]]]
         x_scales = [sb.tile([P, S], U8, name="xs%d" % z, align_bytes=64) for z in range(2)]
 
         def load_pair(z, u):
@@ -56,10 +63,6 @@ def tile_picked_filmg_silu_e_kernel(tc, xT, w1, w2, w3, offs, cen, pos1, pos2, o
                 nc.sync.dma_start(raw[:], x_rows[z, u, :, :, c0 : c0 + width])
                 if (z, u, i) == (0, 0, 0):
                     nc.sync.dma_start(offs_sb[:], offs)
-                if (z, u, i) == (1, 0, 0):
-                    nc.sync.dma_start(cen_sb[:], cen)
-                    nc.sync.dma_start(pos_sb[0][:], pos1)
-                    nc.sync.dma_start(pos_sb[1][:], pos2)
                 src = raw[:].rearrange("p e t -> p t e")
                 if on_scalar > 0:
                     nc.scalar.copy(window[:, c0 : c0 + on_scalar, :], src[:, 0:on_scalar, :])
@@ -67,17 +70,17 @@ def tile_picked_filmg_silu_e_kernel(tc, xT, w1, w2, w3, offs, cen, pos1, pos2, o
                     nc.vector.tensor_copy(window[:, c0 + on_scalar : c0 + width, :], src[:, on_scalar:width, :])
                 c0 += width
             words = window[:].rearrange("p t e -> p (t e)").bitcast(U32)
-            if u == 1:
-                for a in range(2):
-                    nc.vector.tensor_copy(picked[z][:, a, u, :], words.indirect(offs_sb[:, 32 * a : 32 * (a + 1)]))
+            if (z, u) == (0, 0):
+                nc.vector.tensor_copy(picked0[:, :, u, :], words.indirect(offs_sb[:]))
             else:
-                nc.vector.tensor_copy(picked[z][:, :, u, :], words.indirect(offs_sb[:]))
+                for a in range(2):
+                    nc.vector.tensor_copy(picked[z][a][:, u, :], words.indirect(offs_sb[:, 32 * a : 32 * (a + 1)]))
 
-        def weave(z, a0, a1, on_scalar, tag):
-            grouped = sb.tile([P, 4 * HALF * (a1 - a0)], BF16, name="grouped%d%d" % (z, a0), tag=tag, align_bytes=64)
+        def weave(z, a, on_scalar, tag):
+            grouped = sb.tile([P, 4 * HALF], BF16, name="grouped%d%d" % (z, a), tag=tag, align_bytes=64)
             dt = U32 if on_scalar else I32
-            dst = grouped[:].bitcast(dt).rearrange("p (a n u) -> p a n u", n=HALF, u=2)
-            src = picked[z][:, a0:a1, :, :].bitcast(dt).rearrange("p a u n -> p a n u")
+            dst = grouped[:].bitcast(dt).rearrange("p (n u) -> p n u", u=2)
+            src = picked[z][a].bitcast(dt).rearrange("p u n -> p n u")
             if on_scalar:
                 nc.scalar.copy(dst, src)
             else:
@@ -85,16 +88,18 @@ def tile_picked_filmg_silu_e_kernel(tc, xT, w1, w2, w3, offs, cen, pos1, pos2, o
             return grouped
 
         def quantize_x(z, a, grouped, n0, n1):
-            cols = slice(a * HALF + n0, a * HALF + n1)
-            nc.vector.quantize_mx(out=x_codes[z][:, cols].bitcast(FP8X4), scales=x_scales[z][:, cols], in_=grouped[:, 4 * n0 : 4 * n1])
+            nc.vector.quantize_mx(
+                out=x_codes[z][a][:, n0:n1].bitcast(FP8X4),
+                scales=x_scales[z][:, a * HALF + n0 : a * HALF + n1],
+                in_=grouped[:, 4 * n0 : 4 * n1],
+            )
 
         def load_w(name, w):
             raw = sb.tile([P, 2, 4, N], F32, name="raw_" + name, tag="raw_" + name, align_bytes=64)
             nc.sync.dma_start(raw[:], w.rearrange("(z p j) n -> p z j n", z=2, p=P, j=4))
             return raw
 
-        def cast_w(name, raw, on_scalar, tag):
-            grouped = sb.tile([P, 2, N, 4], BF16, name="grouped_" + name, tag=tag, align_bytes=64)
+        def cast_w(grouped, raw, on_scalar):
             dst = grouped[:].rearrange("p z (c i) j -> p z c j i", i=4)
             src = raw[:].rearrange("p z j (c i) -> p z c j i", i=4)
             if on_scalar:
@@ -109,17 +114,17 @@ def tile_picked_filmg_silu_e_kernel(tc, xT, w1, w2, w3, offs, cen, pos1, pos2, o
             nc.vector.quantize_mx(out=codes[:].bitcast(FP8X4), scales=scales[:], in_=grouped[:].rearrange("p z n j -> p (z n j)"))
             return codes, scales
 
-        def product(name, wq, parts, tag):
+        def product(name, wq, parts, order, tag):
             codes, scales = wq
             res = sb.tile([P, S], F32, name="res_" + name, tag=tag, align_bytes=64)
             acc = [ps.tile([P, c1 - c0], F32, name="acc_%s%d" % (name, c0)) for c0, c1, on_scalar in parts]
-            for z in range(2):
-                for bank, (c0, c1, on_scalar) in zip(acc, parts):
+            for z, i in order:
+                for bank, (c0, c1, on_scalar) in [(acc[i], parts[i])]:
                     nc.tensor.matmul_mx(
                         out=bank[:],
                         lhsT=codes[:, z * N : (z + 1) * N].bitcast(FP8X4),
                         lhsT_scale=scales[:, z * N : (z + 1) * N],
-                        rhs=x_codes[z][:, c0:c1].bitcast(FP8X4),
+                        rhs=x_codes[z][c0 // HALF][:, c0 % HALF : c0 % HALF + c1 - c0].bitcast(FP8X4),
                         rhs_scale=x_scales[z][:, c0:c1],
                         start=(z == 0),
                         stop=(z == 1),
@@ -133,28 +138,32 @@ def tile_picked_filmg_silu_e_kernel(tc, xT, w1, w2, w3, offs, cen, pos1, pos2, o
 
         load_pair(0, 0)
         load_pair(0, 1)
-        gx = [weave(0, a, a + 1, False, "gx0%d" % a) for a in range(2)]
+        gx = [weave(0, a, False, "gx0%d" % a) for a in range(2)]
         for a in range(2):
             quantize_x(0, a, gx[a], 0, HALF)
         load_pair(1, 0)
-        raw1 = load_w("w1", w1)
-        g1 = cast_w("w1", raw1, True, "grouped_w1")
-        q1 = quantize_w("w1", g1, "codes_w1")
         load_pair(1, 1)
+        raw1 = load_w("w1", w1)
         raw3 = load_w("w3", w3)
         raw2 = load_w("w2", w2)
-        g3 = cast_w("w3", raw3, True, "grouped_w3")
-        ga = weave(1, 0, 1, False, "gx10")
-        gb = weave(1, 1, 2, True, "raw_w3")
+        nc.sync.dma_start(cen_sb[:], cen)
+        nc.sync.dma_start(pos_sb[0][:], pos1)
+        nc.sync.dma_start(pos_sb[1][:], pos2)
+        g1 = cast_w(sb.tile([P, 2, N, 4], BF16, name="g1", tag="grouped_w1", align_bytes=64), raw1, True)
+        q1 = quantize_w("w1", g1, "codes_w1")
+        ga = weave(1, 0, True, "raw_w1")
+        gb = weave(1, 1, False, "grouped_w1")
+        g3 = cast_w(shared.tile([P, 2, N, 4], BF16, name="g3", offset=0, align_bytes=64), raw3, True)
         quantize_x(1, 0, ga, 0, HALF)
         quantize_x(1, 1, gb, 0, HALF // 2)
         quantize_x(1, 1, gb, HALF // 2, HALF)
-        g2 = cast_w("w2", raw2, True, "picked1")
-        g_sb = product("g", q1, [(0, 512, True), (512, 768, False), (768, 1024, False)], "raw_w2")
-        q3 = quantize_w("w3", g3, "raw_w3")
+        g2 = cast_w(sb.tile([P, 2, N, 4], BF16, name="g2", align_bytes=64), raw2, True)
+        g_sb = product("g", q1, [(0, 512, True), (512, 768, False), (768, 1024, True)], [(0, 0), (0, 1), (0, 2), (1, 0), (1, 1), (1, 2)], "res_g")
+        q3 = quantize_w("w3", g3, "codes_w3")
         q2 = quantize_w("w2", g2, "codes_w2")
-        h_sb = product("h", q3, [(0, 512, True), (512, 1024, True)], "res_h")
-        s_sb = product("s", q2, [(0, 512, True), (512, 1024, True)], "res_s")
+        halves = [(0, 512, True), (512, 1024, True)]
+        h_sb = product("h", q3, halves, [(0, 0), (1, 0), (0, 1), (1, 1)], "res_h")
+        s_sb = product("s", q2, halves, [(0, 0), (1, 0), (0, 1), (1, 1)], "res_s")
 
         gc = sb.tile([P, V], F32, name="gc")
         sc = sb.tile([P, V], F32, name="sc")

@@ -1,7 +1,6 @@
 from contextlib import ExitStack
 
 import concourse.mybir as mybir
-from concourse.masks import make_identity
 
 K, T, S, V, N = 1024, 2048, 1024, 512, 128
 FLOPS = 3 * 2 * K * S * N
@@ -19,8 +18,7 @@ SILU = mybir.ActivationFunctionType.Silu
 
 P = 128
 HALF = 512
-CHUNKS = [[(2048, 704)], [(1024, 1024), (1024, 384)], [(1024, 1024), (1024, 576)], [(1024, 1024), (512, 0), (512, 176)]]
-TAIL = "v"
+CHUNKS = [[(2048, 704)], [(1024, 1024), (1024, 320)], [(768, 768), (768, 768), (512, 0)], [(768, 768), (768, 400), (512, 176)]]
 PIECES = [192, 192, 128]
 
 
@@ -40,9 +38,6 @@ def tile_picked_filmg_silu_e_kernel(tc, xT, w1, w2, w3, offs, cen, pos1, pos2, o
         warm_out = sb.tile([P, 8], F32, name="warm_out")
         nc.gpsimd.memset(warm_in[:], 0.0)
         nc.scalar.activation(warm_out[:], warm_in[:], SILU)
-        if TAIL == "pe":
-            ident = sb.tile([P, P], F32, name="ident")
-            make_identity(nc, ident[:])
 
         x_rows = xT.rearrange("(z p u e) t -> z u p e t", z=2, p=P, u=2, e=2)
         picked0 = sb.tile([P, 2, 2, HALF], U32, name="picked0")
@@ -59,7 +54,7 @@ def tile_picked_filmg_silu_e_kernel(tc, xT, w1, w2, w3, offs, cen, pos1, pos2, o
             window = sb.tile([P, T, 2], BF16, name="window%d%d" % (z, u))
             c0 = 0
             for i, (width, on_scalar) in enumerate(CHUNKS[2 * z + u]):
-                raw = sb.tile([P, 2, width], F32, name="raw%d%d%d" % (z, u, i))
+                raw = sb.tile([P, 2, width], F32, name="raw%d%d%d" % (z, u, i), tag="raw%d%d%d" % (z, u, i), align_bytes=64)
                 nc.sync.dma_start(raw[:], x_rows[z, u, :, :, c0 : c0 + width])
                 if (z, u, i) == (0, 0, 0):
                     nc.sync.dma_start(offs_sb[:], offs)
@@ -138,10 +133,9 @@ def tile_picked_filmg_silu_e_kernel(tc, xT, w1, w2, w3, offs, cen, pos1, pos2, o
 
         load_pair(0, 0)
         load_pair(0, 1)
-        gx = [weave(0, a, False, "gx0%d" % a) for a in range(2)]
-        for a in range(2):
-            quantize_x(0, a, gx[a], 0, HALF)
+        quantize_x(0, 0, weave(0, 0, False, "gx00"), 0, HALF)
         load_pair(1, 0)
+        quantize_x(0, 1, weave(0, 1, True, "raw101"), 0, HALF)
         load_pair(1, 1)
         raw1 = load_w("w1", w1)
         raw3 = load_w("w3", w3)

@@ -18,7 +18,7 @@ SILU = mybir.ActivationFunctionType.Silu
 
 P = 128
 HALF = 512
-CHUNKS = [[(2048, 704)], [(1024, 1024), (1024, 320)], [(768, 768), (768, 768), (512, 0)], [(768, 768), (768, 400), (512, 176)]]
+CHUNKS = [[(1536, 544), (512, 176)], [(768, 768), (768, 256), (512, 176)], [(768, 768), (768, 768), (512, 0)], [(768, 768), (768, 320), (512, 176)]]
 PIECES = [192, 192, 128]
 
 
@@ -28,16 +28,17 @@ def tile_picked_filmg_silu_e_kernel(tc, xT, w1, w2, w3, offs, cen, pos1, pos2, o
         lists = ctx.enter_context(tc.tile_pool(name="lists", bufs=1))
         sb = ctx.enter_context(tc.tile_pool(name="sb", bufs=1))
         shared = ctx.enter_context(tc.tile_pool(name="shared", bufs=1))
+        late = ctx.enter_context(tc.tile_pool(name="late", bufs=1))
         ps = ctx.enter_context(tc.psum_pool(name="ps", bufs=1))
 
         offs_sb = lists.tile([P, S // 16], U16, name="offs_sb")
         cen_sb = lists.tile([P, V // 16], U16, name="cen_sb")
         pos_sb = [lists.tile([P, V // 16], U16, name="pos%d_sb" % d) for d in range(2)]
 
-        warm_in = sb.tile([P, 8], F32, name="warm_in")
-        warm_out = sb.tile([P, 8], F32, name="warm_out")
-        nc.gpsimd.memset(warm_in[:], 0.0)
-        nc.scalar.activation(warm_out[:], warm_in[:], SILU)
+        zero_in = sb.tile([P, 1], F32, name="zero_in")
+        zero = sb.tile([P, 1], F32, name="zero")
+        nc.gpsimd.memset(zero_in[:], 0.0)
+        nc.scalar.activation(zero[:], zero_in[:], SILU)
 
         x_rows = xT.rearrange("(z p u e) t -> z u p e t", z=2, p=P, u=2, e=2)
         picked0 = sb.tile([P, 2, 2, HALF], U32, name="picked0")
@@ -72,7 +73,10 @@ def tile_picked_filmg_silu_e_kernel(tc, xT, w1, w2, w3, offs, cen, pos1, pos2, o
                     nc.vector.tensor_copy(picked[z][a][:, u, :], words.indirect(offs_sb[:, 32 * a : 32 * (a + 1)]))
 
         def weave(z, a, on_scalar, tag):
-            grouped = sb.tile([P, 4 * HALF], BF16, name="grouped%d%d" % (z, a), tag=tag, align_bytes=64)
+            if z == 1:
+                grouped = late.tile([P, 4 * HALF], BF16, name="grouped%d%d" % (z, a), offset=4096 * a, align_bytes=64)
+            else:
+                grouped = sb.tile([P, 4 * HALF], BF16, name="grouped%d%d" % (z, a), tag=tag, align_bytes=64)
             dt = U32 if on_scalar else I32
             dst = grouped[:].bitcast(dt).rearrange("p (n u) -> p n u", u=2)
             src = picked[z][a].bitcast(dt).rearrange("p u n -> p n u")
@@ -90,7 +94,10 @@ def tile_picked_filmg_silu_e_kernel(tc, xT, w1, w2, w3, offs, cen, pos1, pos2, o
             )
 
         def load_w(name, w):
-            raw = sb.tile([P, 2, 4, N], F32, name="raw_" + name, tag="raw_" + name, align_bytes=64)
+            if name == "w1":
+                raw = late.tile([P, 2, 4, N], F32, name="raw_w1", offset=2048, align_bytes=64)
+            else:
+                raw = sb.tile([P, 2, 4, N], F32, name="raw_" + name, align_bytes=64)
             nc.sync.dma_start(raw[:], w.rearrange("(z p j) n -> p z j n", z=2, p=P, j=4))
             return raw
 
@@ -135,7 +142,7 @@ def tile_picked_filmg_silu_e_kernel(tc, xT, w1, w2, w3, offs, cen, pos1, pos2, o
         load_pair(0, 1)
         quantize_x(0, 0, weave(0, 0, False, "gx00"), 0, HALF)
         load_pair(1, 0)
-        quantize_x(0, 1, weave(0, 1, True, "raw101"), 0, HALF)
+        quantize_x(0, 1, weave(0, 1, True, "raw102"), 0, HALF)
         load_pair(1, 1)
         raw1 = load_w("w1", w1)
         raw3 = load_w("w3", w3)
@@ -163,8 +170,9 @@ def tile_picked_filmg_silu_e_kernel(tc, xT, w1, w2, w3, offs, cen, pos1, pos2, o
         sc = sb.tile([P, V], F32, name="sc")
         nc.vector.tensor_copy(gc[:], g_sb[:].indirect(cen_sb[:]))
         prod = sb.tile([P, 2, V], F32, name="prod")
-        for d in range(2):
-            nc.vector.tensor_tensor(prod[:, d, :], h_sb[:].indirect(pos_sb[d][:]), gc[:], MULT)
+        nc.vector.tensor_tensor(prod[:, 0, :], h_sb[:].indirect(pos_sb[0][:]), gc[:], MULT)
+        for v0, v1 in ((0, PIECES[0]), (PIECES[0], V)):
+            nc.vector.tensor_tensor(prod[:, 1, v0:v1], h_sb[:].indirect(pos_sb[1][:, v0 // 16 : v1 // 16]), gc[:, v0:v1], MULT)
         nc.vector.tensor_copy(sc[:], s_sb[:].indirect(cen_sb[:]))
         acts = []
         v0 = 0
@@ -173,7 +181,7 @@ def tile_picked_filmg_silu_e_kernel(tc, xT, w1, w2, w3, offs, cen, pos1, pos2, o
             pre = sb.tile([P, 2, width], F32, name="pre%d" % i)
             act = sb.tile([P, 2, width], F32, name="act%d" % i)
             nc.vector.tensor_tensor(pre[:], prod[:, :, cols], sc[:, cols].unsqueeze(1).to_broadcast([P, 2, width]), ADD)
-            nc.scalar.activation(act[:], pre[:], SILU)
+            nc.scalar.activation(act[:], pre[:], SILU, bias=zero[:])
             acts.append(act)
             v0 += width
         v0 = 0

@@ -18,7 +18,7 @@ SILU = mybir.ActivationFunctionType.Silu
 
 P = 128
 HALF = 512
-CHUNKS = [[(1536, 544), (512, 176)], [(768, 768), (768, 256), (512, 176)], [(768, 768), (768, 768), (512, 0)], [(768, 768), (768, 320), (512, 176)]]
+CHUNKS = [[(2048, 704)], [(1024, 1024), (1024, 320)], [(768, 768), (768, 768), (512, 0)], [(768, 768), (768, 480), (512, 176)]]
 PIECES = [192, 192, 128]
 
 

@@ -17,9 +17,20 @@ ADD = mybir.AluOpType.add
 SILU = mybir.ActivationFunctionType.Silu
 
 P = 128
-HALF = 512
-CHUNKS = [[(2048, 704)], [(1024, 1024), (1024, 320)], [(768, 768), (768, 768), (512, 0)], [(768, 768), (768, 480), (512, 176)]]
+PER_COLUMN = 16
+HALF = S // 2
+QUARTER = S // 4
+
+LOADS = [
+    [(2048, 704)],
+    [(1280, 896), (768, 208)],
+    [(768, 768), (768, 768), (512, 0)],
+    [(768, 768), (768, 400), (512, 176)],
+]
 PIECES = [192, 192, 128]
+
+WOVEN_BYTES = 4 * HALF * 2
+W_BF16_BYTES = 2 * N * 4 * 2
 
 
 def tile_picked_filmg_silu_e_kernel(tc, xT, w1, w2, w3, offs, cen, pos1, pos2, out):
@@ -27,13 +38,13 @@ def tile_picked_filmg_silu_e_kernel(tc, xT, w1, w2, w3, offs, cen, pos1, pos2, o
     with ExitStack() as ctx:
         lists = ctx.enter_context(tc.tile_pool(name="lists", bufs=1))
         sb = ctx.enter_context(tc.tile_pool(name="sb", bufs=1))
-        shared = ctx.enter_context(tc.tile_pool(name="shared", bufs=1))
-        late = ctx.enter_context(tc.tile_pool(name="late", bufs=1))
+        after_weave = ctx.enter_context(tc.tile_pool(name="after_weave", bufs=1))
+        after_w1 = ctx.enter_context(tc.tile_pool(name="after_w1", bufs=1))
         ps = ctx.enter_context(tc.psum_pool(name="ps", bufs=1))
 
-        offs_sb = lists.tile([P, S // 16], U16, name="offs_sb")
-        cen_sb = lists.tile([P, V // 16], U16, name="cen_sb")
-        pos_sb = [lists.tile([P, V // 16], U16, name="pos%d_sb" % d) for d in range(2)]
+        offs_sb = lists.tile([P, S // PER_COLUMN], U16, name="offs_sb")
+        cen_sb = lists.tile([P, V // PER_COLUMN], U16, name="cen_sb")
+        pos_sb = [lists.tile([P, V // PER_COLUMN], U16, name="pos%d_sb" % d) for d in range(2)]
 
         zero_in = sb.tile([P, 1], F32, name="zero_in")
         zero = sb.tile([P, 1], F32, name="zero")
@@ -42,129 +53,120 @@ def tile_picked_filmg_silu_e_kernel(tc, xT, w1, w2, w3, offs, cen, pos1, pos2, o
 
         x_rows = xT.rearrange("(z p u e) t -> z u p e t", z=2, p=P, u=2, e=2)
         picked0 = sb.tile([P, 2, 2, HALF], U32, name="picked0")
-        picked1a = shared.tile([P, 2, HALF], U32, name="picked1a", offset=0, align_bytes=64)
+        picked1a = after_weave.tile([P, 2, HALF], U32, name="picked1a", offset=0, align_bytes=64)
         picked1b = sb.tile([P, 2, HALF], U32, name="picked1b")
         picked = [[picked0[:, 0], picked0[:, 1]], [picked1a[:], picked1b[:]]]
         x_codes0 = sb.tile([P, S], U32, name="xc0", align_bytes=64)
         x_codes1a = sb.tile([P, HALF], U32, name="xc1a", align_bytes=64)
-        x_codes1b = shared.tile([P, HALF], U32, name="xc1b", offset=2048, align_bytes=64)
+        x_codes1b = after_weave.tile([P, HALF], U32, name="xc1b", offset=W_BF16_BYTES, align_bytes=64)
         x_codes = [[x_codes0[:, 0:HALF], x_codes0[:, HALF:S]], [x_codes1a[:], x_codes1b[:]]]
         x_scales = [sb.tile([P, S], U8, name="xs%d" % z, align_bytes=64) for z in range(2)]
 
-        def load_pair(z, u):
-            window = sb.tile([P, T, 2], BF16, name="window%d%d" % (z, u))
-            c0 = 0
-            for i, (width, on_scalar) in enumerate(CHUNKS[2 * z + u]):
-                raw = sb.tile([P, 2, width], F32, name="raw%d%d%d" % (z, u, i), tag="raw%d%d%d" % (z, u, i), align_bytes=64)
-                nc.sync.dma_start(raw[:], x_rows[z, u, :, :, c0 : c0 + width])
-                if (z, u, i) == (0, 0, 0):
-                    nc.sync.dma_start(offs_sb[:], offs)
-                src = raw[:].rearrange("p e t -> p t e")
-                if on_scalar > 0:
-                    nc.scalar.copy(window[:, c0 : c0 + on_scalar, :], src[:, 0:on_scalar, :])
-                if on_scalar < width:
-                    nc.vector.tensor_copy(window[:, c0 + on_scalar : c0 + width, :], src[:, on_scalar:width, :])
-                c0 += width
-            words = window[:].rearrange("p t e -> p (t e)").bitcast(U32)
-            if (z, u) == (0, 0):
-                nc.vector.tensor_copy(picked0[:, :, u, :], words.indirect(offs_sb[:]))
-            else:
-                for a in range(2):
-                    nc.vector.tensor_copy(picked[z][a][:, u, :], words.indirect(offs_sb[:, 32 * a : 32 * (a + 1)]))
-
-        def weave(z, a, on_scalar, tag):
-            if z == 1:
-                grouped = late.tile([P, 4 * HALF], BF16, name="grouped%d%d" % (z, a), offset=4096 * a, align_bytes=64)
-            else:
-                grouped = sb.tile([P, 4 * HALF], BF16, name="grouped%d%d" % (z, a), tag=tag, align_bytes=64)
-            dt = U32 if on_scalar else I32
-            dst = grouped[:].bitcast(dt).rearrange("p (n u) -> p n u", u=2)
-            src = picked[z][a].bitcast(dt).rearrange("p u n -> p n u")
+        def move(on_scalar, dst, src):
             if on_scalar:
                 nc.scalar.copy(dst, src)
             else:
                 nc.vector.tensor_copy(dst, src)
-            return grouped
 
-        def quantize_x(z, a, grouped, n0, n1):
+        def load_pair(z, u):
+            first_pair = (z, u) == (0, 0)
+            window = sb.tile([P, T, 2], BF16, name="window%d%d" % (z, u))
+            c0 = 0
+            for i, (width, scalar_cols) in enumerate(LOADS[2 * z + u]):
+                raw = sb.tile([P, 2, width], F32, name="raw%d%d%d" % (z, u, i), tag="raw%d%d%d" % (z, u, i), align_bytes=64)
+                nc.sync.dma_start(raw[:], x_rows[z, u, :, :, c0 : c0 + width])
+                if first_pair:
+                    nc.sync.dma_start(offs_sb[:], offs)
+                src = raw[:].rearrange("p e t -> p t e")
+                if scalar_cols > 0:
+                    nc.scalar.copy(window[:, c0 : c0 + scalar_cols, :], src[:, 0:scalar_cols, :])
+                if scalar_cols < width:
+                    nc.vector.tensor_copy(window[:, c0 + scalar_cols : c0 + width, :], src[:, scalar_cols:width, :])
+                c0 += width
+            words = window[:].rearrange("p t e -> p (t e)").bitcast(U32)
+            if first_pair:
+                nc.vector.tensor_copy(picked0[:, :, u, :], words.indirect(offs_sb[:]))
+            else:
+                cols = HALF // PER_COLUMN
+                for a in range(2):
+                    nc.vector.tensor_copy(picked[z][a][:, u, :], words.indirect(offs_sb[:, cols * a : cols * (a + 1)]))
+
+        def weave(woven, z, a, on_scalar):
+            dt = U32 if on_scalar else I32
+            move(on_scalar, woven[:].bitcast(dt).rearrange("p (n u) -> p n u", u=2), picked[z][a].bitcast(dt).rearrange("p u n -> p n u"))
+            return woven
+
+        def quantize_x(z, a, woven, n0, n1):
             nc.vector.quantize_mx(
                 out=x_codes[z][a][:, n0:n1].bitcast(FP8X4),
                 scales=x_scales[z][:, a * HALF + n0 : a * HALF + n1],
-                in_=grouped[:, 4 * n0 : 4 * n1],
+                in_=woven[:, 4 * n0 : 4 * n1],
             )
 
-        def load_w(name, w):
-            if name == "w1":
-                raw = late.tile([P, 2, 4, N], F32, name="raw_w1", offset=2048, align_bytes=64)
-            else:
-                raw = sb.tile([P, 2, 4, N], F32, name="raw_" + name, align_bytes=64)
+        def load_w(raw, w):
             nc.sync.dma_start(raw[:], w.rearrange("(z p j) n -> p z j n", z=2, p=P, j=4))
             return raw
 
-        def cast_w(grouped, raw, on_scalar):
-            dst = grouped[:].rearrange("p z (c i) j -> p z c j i", i=4)
-            src = raw[:].rearrange("p z j (c i) -> p z c j i", i=4)
-            if on_scalar:
-                nc.scalar.copy(dst, src)
-            else:
-                nc.vector.tensor_copy(dst, src)
-            return grouped
+        def round_w(rounded, raw):
+            nc.scalar.copy(rounded[:].rearrange("p z (c i) j -> p z c j i", i=4), raw[:].rearrange("p z j (c i) -> p z c j i", i=4))
+            return rounded
 
-        def quantize_w(name, grouped, tag):
-            codes = sb.tile([P, 2 * N], U32, name="codes_" + name, tag=tag, align_bytes=64)
+        def quantize_w(name, rounded):
+            codes = sb.tile([P, 2 * N], U32, name="codes_" + name, align_bytes=64)
             scales = sb.tile([P, 2 * N], U8, name="scales_" + name, align_bytes=64)
-            nc.vector.quantize_mx(out=codes[:].bitcast(FP8X4), scales=scales[:], in_=grouped[:].rearrange("p z n j -> p (z n j)"))
+            nc.vector.quantize_mx(out=codes[:].bitcast(FP8X4), scales=scales[:], in_=rounded[:].rearrange("p z n j -> p (z n j)"))
             return codes, scales
 
-        def product(name, wq, parts, order, tag):
-            codes, scales = wq
-            res = sb.tile([P, S], F32, name="res_" + name, tag=tag, align_bytes=64)
-            acc = [ps.tile([P, c1 - c0], F32, name="acc_%s%d" % (name, c0)) for c0, c1, on_scalar in parts]
+        def product(name, quantized_w, parts, order):
+            codes, scales = quantized_w
+            res = sb.tile([P, S], F32, name="res_" + name, align_bytes=64)
+            banks = [ps.tile([P, c1 - c0], F32, name="acc_%s%d" % (name, c0)) for c0, c1, on_scalar in parts]
             for z, i in order:
-                for bank, (c0, c1, on_scalar) in [(acc[i], parts[i])]:
-                    nc.tensor.matmul_mx(
-                        out=bank[:],
-                        lhsT=codes[:, z * N : (z + 1) * N].bitcast(FP8X4),
-                        lhsT_scale=scales[:, z * N : (z + 1) * N],
-                        rhs=x_codes[z][c0 // HALF][:, c0 % HALF : c0 % HALF + c1 - c0].bitcast(FP8X4),
-                        rhs_scale=x_scales[z][:, c0:c1],
-                        start=(z == 0),
-                        stop=(z == 1),
-                    )
-            for bank, (c0, c1, on_scalar) in zip(acc, parts):
-                if on_scalar:
-                    nc.scalar.copy(res[:, c0:c1], bank[:])
-                else:
-                    nc.vector.tensor_copy(res[:, c0:c1], bank[:])
+                c0, c1, on_scalar = parts[i]
+                nc.tensor.matmul_mx(
+                    out=banks[i][:],
+                    lhsT=codes[:, z * N : (z + 1) * N].bitcast(FP8X4),
+                    lhsT_scale=scales[:, z * N : (z + 1) * N],
+                    rhs=x_codes[z][c0 // HALF][:, c0 % HALF : c0 % HALF + c1 - c0].bitcast(FP8X4),
+                    rhs_scale=x_scales[z][:, c0:c1],
+                    start=(z == 0),
+                    stop=(z == 1),
+                )
+            for bank, (c0, c1, on_scalar) in zip(banks, parts):
+                move(on_scalar, res[:, c0:c1], bank[:])
             return res
 
         load_pair(0, 0)
         load_pair(0, 1)
-        quantize_x(0, 0, weave(0, 0, False, "gx00"), 0, HALF)
+        woven00 = sb.tile([P, 4 * HALF], BF16, name="woven00", align_bytes=64)
+        quantize_x(0, 0, weave(woven00, 0, 0, False), 0, HALF)
         load_pair(1, 0)
-        quantize_x(0, 1, weave(0, 1, True, "raw102"), 0, HALF)
+        woven01 = sb.tile([P, 4 * HALF], BF16, name="woven01", tag="raw10%d" % (len(LOADS[2]) - 1), align_bytes=64)
+        quantize_x(0, 1, weave(woven01, 0, 1, True), 0, HALF)
         load_pair(1, 1)
-        raw1 = load_w("w1", w1)
-        raw3 = load_w("w3", w3)
-        raw2 = load_w("w2", w2)
+
+        raw1 = load_w(after_w1.tile([P, 2, 4, N], F32, name="raw_w1", offset=WOVEN_BYTES // 2, align_bytes=64), w1)
+        raw3 = load_w(sb.tile([P, 2, 4, N], F32, name="raw_w3", align_bytes=64), w3)
+        raw2 = load_w(sb.tile([P, 2, 4, N], F32, name="raw_w2", align_bytes=64), w2)
         nc.sync.dma_start(cen_sb[:], cen)
         nc.sync.dma_start(pos_sb[0][:], pos1)
         nc.sync.dma_start(pos_sb[1][:], pos2)
-        g1 = cast_w(sb.tile([P, 2, N, 4], BF16, name="g1", tag="grouped_w1", align_bytes=64), raw1, True)
-        q1 = quantize_w("w1", g1, "codes_w1")
-        ga = weave(1, 0, True, "raw_w1")
-        gb = weave(1, 1, False, "grouped_w1")
-        g3 = cast_w(shared.tile([P, 2, N, 4], BF16, name="g3", offset=0, align_bytes=64), raw3, True)
-        quantize_x(1, 0, ga, 0, HALF)
-        quantize_x(1, 1, gb, 0, HALF // 2)
-        quantize_x(1, 1, gb, HALF // 2, HALF)
-        g2 = cast_w(sb.tile([P, 2, N, 4], BF16, name="g2", align_bytes=64), raw2, True)
-        g_sb = product("g", q1, [(0, 512, True), (512, 768, False), (768, 1024, True)], [(0, 0), (0, 1), (0, 2), (1, 0), (1, 1), (1, 2)], "res_g")
-        q3 = quantize_w("w3", g3, "codes_w3")
-        q2 = quantize_w("w2", g2, "codes_w2")
-        halves = [(0, 512, True), (512, 1024, True)]
-        h_sb = product("h", q3, halves, [(0, 0), (1, 0), (0, 1), (1, 1)], "res_h")
-        s_sb = product("s", q2, halves, [(0, 0), (1, 0), (0, 1), (1, 1)], "res_s")
+        q1 = quantize_w("w1", round_w(sb.tile([P, 2, N, 4], BF16, name="rounded_w1", align_bytes=64), raw1))
+        woven10 = weave(after_w1.tile([P, 4 * HALF], BF16, name="woven10", offset=0, align_bytes=64), 1, 0, True)
+        woven11 = weave(after_w1.tile([P, 4 * HALF], BF16, name="woven11", offset=WOVEN_BYTES, align_bytes=64), 1, 1, False)
+        rounded3 = round_w(after_weave.tile([P, 2, N, 4], BF16, name="rounded_w3", offset=0, align_bytes=64), raw3)
+        quantize_x(1, 0, woven10, 0, HALF)
+        quantize_x(1, 1, woven11, 0, QUARTER)
+        quantize_x(1, 1, woven11, QUARTER, HALF)
+        rounded2 = round_w(sb.tile([P, 2, N, 4], BF16, name="rounded_w2", align_bytes=64), raw2)
+        g_parts = [(0, HALF, True), (HALF, HALF + QUARTER, False), (HALF + QUARTER, S, True)]
+        g_sb = product("g", q1, g_parts, [(z, i) for z in range(2) for i in range(len(g_parts))])
+        q3 = quantize_w("w3", rounded3)
+        q2 = quantize_w("w2", rounded2)
+        halves = [(0, HALF, True), (HALF, S, True)]
+        half_by_half = [(z, i) for i in range(2) for z in range(2)]
+        h_sb = product("h", q3, halves, half_by_half)
+        s_sb = product("s", q2, halves, half_by_half)
 
         gc = sb.tile([P, V], F32, name="gc")
         sc = sb.tile([P, V], F32, name="sc")
@@ -172,8 +174,9 @@ def tile_picked_filmg_silu_e_kernel(tc, xT, w1, w2, w3, offs, cen, pos1, pos2, o
         prod = sb.tile([P, 2, V], F32, name="prod")
         nc.vector.tensor_tensor(prod[:, 0, :], h_sb[:].indirect(pos_sb[0][:]), gc[:], MULT)
         for v0, v1 in ((0, PIECES[0]), (PIECES[0], V)):
-            nc.vector.tensor_tensor(prod[:, 1, v0:v1], h_sb[:].indirect(pos_sb[1][:, v0 // 16 : v1 // 16]), gc[:, v0:v1], MULT)
+            nc.vector.tensor_tensor(prod[:, 1, v0:v1], h_sb[:].indirect(pos_sb[1][:, v0 // PER_COLUMN : v1 // PER_COLUMN]), gc[:, v0:v1], MULT)
         nc.vector.tensor_copy(sc[:], s_sb[:].indirect(cen_sb[:]))
+
         acts = []
         v0 = 0
         for i, width in enumerate(PIECES):
@@ -187,7 +190,7 @@ def tile_picked_filmg_silu_e_kernel(tc, xT, w1, w2, w3, offs, cen, pos1, pos2, o
         v0 = 0
         for i, width in enumerate(PIECES):
             cols = slice(v0, v0 + width)
-            res = sb.tile([P, width], F32, name="res%d" % i)
-            nc.vector.tensor_tensor(res[:], acts[i][:, 0, :], acts[i][:, 1, :], ADD)
-            nc.sync.dma_start(out[:, cols], res[:])
+            total = sb.tile([P, width], F32, name="total%d" % i)
+            nc.vector.tensor_tensor(total[:], acts[i][:, 0, :], acts[i][:, 1, :], ADD)
+            nc.sync.dma_start(out[:, cols], total[:])
             v0 += width

@@ -22,10 +22,10 @@ HALF = S // 2
 QUARTER = S // 4
 
 LOADS = [
-    [(2048, 704)],
-    [(1280, 896), (768, 208)],
-    [(768, 768), (768, 768), (512, 0)],
-    [(768, 768), (768, 400), (512, 176)],
+    [(2048, 704, 0)],
+    [(1280, 832, 448), (768, 224, 0)],
+    [(768, 128, 640), (768, 352, 0), (512, 0, 0)],
+    [(768, 320, 448), (768, 576, 192), (512, 176, 0)],
 ]
 PIECES = [192, 192, 128]
 
@@ -56,10 +56,10 @@ def tile_picked_filmg_silu_e_kernel(tc, xT, w1, w2, w3, offs, cen, pos1, pos2, o
         picked1a = after_weave.tile([P, 2, HALF], U32, name="picked1a", offset=0, align_bytes=64)
         picked1b = sb.tile([P, 2, HALF], U32, name="picked1b")
         picked = [[picked0[:, 0], picked0[:, 1]], [picked1a[:], picked1b[:]]]
-        x_codes0 = sb.tile([P, S], U32, name="xc0", align_bytes=64)
+        x_codes0a = sb.tile([P, HALF], U32, name="xc0a", align_bytes=64)
         x_codes1a = sb.tile([P, HALF], U32, name="xc1a", align_bytes=64)
         x_codes1b = after_weave.tile([P, HALF], U32, name="xc1b", offset=W_BF16_BYTES, align_bytes=64)
-        x_codes = [[x_codes0[:, 0:HALF], x_codes0[:, HALF:S]], [x_codes1a[:], x_codes1b[:]]]
+        x_codes = [[x_codes0a[:]], [x_codes1a[:], x_codes1b[:]]]
         x_scales = [sb.tile([P, S], U8, name="xs%d" % z, align_bytes=64) for z in range(2)]
 
         def move(on_scalar, dst, src):
@@ -68,11 +68,11 @@ def tile_picked_filmg_silu_e_kernel(tc, xT, w1, w2, w3, offs, cen, pos1, pos2, o
             else:
                 nc.vector.tensor_copy(dst, src)
 
-        def load_pair(z, u):
+        def load_pair(z, u, after_first_load=None):
             first_pair = (z, u) == (0, 0)
-            window = sb.tile([P, T, 2], BF16, name="window%d%d" % (z, u))
+            window = sb.tile([P, T, 2], BF16, name="window%d%d" % (z, u), tag="raw102" if (z, u) == (1, 1) else "window%d%d" % (z, u), align_bytes=64)
             c0 = 0
-            for i, (width, scalar_cols) in enumerate(LOADS[2 * z + u]):
+            for i, (width, scalar_cols, gpsimd_cols) in enumerate(LOADS[2 * z + u]):
                 raw = sb.tile([P, 2, width], F32, name="raw%d%d%d" % (z, u, i), tag="raw%d%d%d" % (z, u, i), align_bytes=64)
                 nc.sync.dma_start(raw[:], x_rows[z, u, :, :, c0 : c0 + width])
                 if first_pair:
@@ -80,20 +80,30 @@ def tile_picked_filmg_silu_e_kernel(tc, xT, w1, w2, w3, offs, cen, pos1, pos2, o
                 src = raw[:].rearrange("p e t -> p t e")
                 if scalar_cols > 0:
                     nc.scalar.copy(window[:, c0 : c0 + scalar_cols, :], src[:, 0:scalar_cols, :])
-                if scalar_cols < width:
-                    nc.vector.tensor_copy(window[:, c0 + scalar_cols : c0 + width, :], src[:, scalar_cols:width, :])
+                c1 = scalar_cols + gpsimd_cols
+                if gpsimd_cols > 0:
+                    nc.gpsimd.tensor_scalar(window[:, c0 + scalar_cols : c0 + c1, :], src[:, scalar_cols:c1, :], 1.0, 0.0, MULT, ADD)
+                if c1 < width:
+                    nc.vector.tensor_copy(window[:, c0 + c1 : c0 + width, :], src[:, c1:width, :])
                 c0 += width
+                if i == 0 and after_first_load is not None:
+                    after_first_load()
             words = window[:].rearrange("p t e -> p (t e)").bitcast(U32)
             if first_pair:
                 nc.vector.tensor_copy(picked0[:, :, u, :], words.indirect(offs_sb[:]))
+            elif (z, u) == (0, 1):
+                cols = QUARTER // PER_COLUMN
+                for q in range(4):
+                    n0 = QUARTER * (q % 2)
+                    nc.vector.tensor_copy(picked[z][q // 2][:, u, n0 : n0 + QUARTER], words.indirect(offs_sb[:, cols * q : cols * (q + 1)]))
             else:
                 cols = HALF // PER_COLUMN
                 for a in range(2):
                     nc.vector.tensor_copy(picked[z][a][:, u, :], words.indirect(offs_sb[:, cols * a : cols * (a + 1)]))
 
-        def weave(woven, z, a, on_scalar):
+        def weave(woven, z, a, on_scalar, n0=0, n1=HALF):
             dt = U32 if on_scalar else I32
-            move(on_scalar, woven[:].bitcast(dt).rearrange("p (n u) -> p n u", u=2), picked[z][a].bitcast(dt).rearrange("p u n -> p n u"))
+            move(on_scalar, woven[:, 4 * n0 : 4 * n1].bitcast(dt).rearrange("p (n u) -> p n u", u=2), picked[z][a][:, :, n0:n1].bitcast(dt).rearrange("p u n -> p n u"))
             return woven
 
         def quantize_x(z, a, woven, n0, n1):
@@ -136,14 +146,19 @@ def tile_picked_filmg_silu_e_kernel(tc, xT, w1, w2, w3, offs, cen, pos1, pos2, o
                 move(on_scalar, res[:, c0:c1], bank[:])
             return res
 
+        def late_quantize():
+            x_codes[0].append(sb.tile([P, HALF], U32, name="xc0b", tag="raw110", align_bytes=64)[:])
+            quantize_x(0, 1, woven0[1], 0, HALF)
+
         load_pair(0, 0)
         load_pair(0, 1)
-        woven00 = sb.tile([P, 4 * HALF], BF16, name="woven00", align_bytes=64)
-        quantize_x(0, 0, weave(woven00, 0, 0, False), 0, HALF)
+        woven0 = [sb.tile([P, 4 * HALF], BF16, name="woven0%d" % a, align_bytes=64) for a in range(2)]
+        for a in range(2):
+            weave(woven0[a], 0, a, True, 0, QUARTER)
+            weave(woven0[a], 0, a, True, QUARTER, HALF)
+        quantize_x(0, 0, woven0[0], 0, HALF)
         load_pair(1, 0)
-        woven01 = sb.tile([P, 4 * HALF], BF16, name="woven01", tag="raw10%d" % (len(LOADS[2]) - 1), align_bytes=64)
-        quantize_x(0, 1, weave(woven01, 0, 1, True), 0, HALF)
-        load_pair(1, 1)
+        load_pair(1, 1, late_quantize)
 
         raw1 = load_w(after_w1.tile([P, 2, 4, N], F32, name="raw_w1", offset=WOVEN_BYTES // 2, align_bytes=64), w1)
         raw3 = load_w(sb.tile([P, 2, 4, N], F32, name="raw_w3", align_bytes=64), w3)

@@ -22,10 +22,10 @@ HALF = S // 2
 QUARTER = S // 4
 
 LOADS = [
-    [(2048, 704, 0)],
-    [(1280, 832, 448), (768, 224, 0)],
-    [(768, 128, 640), (768, 352, 0), (512, 0, 0)],
-    [(768, 320, 448), (768, 576, 192), (512, 176, 0)],
+    [(1024, 352, 0), (1024, 352, 0)],
+    [(640, 320, 320), (896, 320, 0), (512, 128, 0)],
+    [(512, 0, 256), (896, 384, 0), (640, 384, 0)],
+    [(896, 384, 512), (768, 448, 320), (384, 128, 0)],
 ]
 PIECES = [192, 192, 128]
 
@@ -52,6 +52,7 @@ def tile_picked_filmg_silu_e_kernel(tc, xT, w1, w2, w3, offs, cen, pos1, pos2, o
         nc.scalar.activation(zero[:], zero_in[:], SILU)
 
         x_rows = xT.rearrange("(z p u e) t -> z u p e t", z=2, p=P, u=2, e=2)
+        x_runs = xT.rearrange("(z p u e) t -> z u p (e t)", z=2, p=P, u=2, e=2)
         picked0 = sb.tile([P, 2, 2, HALF], U32, name="picked0")
         picked1a = after_weave.tile([P, 2, HALF], U32, name="picked1a", offset=0, align_bytes=64)
         picked1b = sb.tile([P, 2, HALF], U32, name="picked1b")
@@ -68,16 +69,24 @@ def tile_picked_filmg_silu_e_kernel(tc, xT, w1, w2, w3, offs, cen, pos1, pos2, o
             else:
                 nc.vector.tensor_copy(dst, src)
 
-        def load_pair(z, u, after_first_load=None):
+        def load_pair(z, u):
             first_pair = (z, u) == (0, 0)
-            window = sb.tile([P, T, 2], BF16, name="window%d%d" % (z, u), tag="raw102" if (z, u) == (1, 1) else "window%d%d" % (z, u), align_bytes=64)
+            window = sb.tile([P, T, 2], BF16, name="window%d%d" % (z, u), tag="raw10" if (z, u) == (1, 1) else "window%d%d" % (z, u), align_bytes=64)
+            last_pair = (z, u) == (1, 1)
+            if not last_pair:
+                run = sb.tile([P, 2 * T], F32, name="raw%d%d" % (z, u), tag="raw%d%d" % (z, u), align_bytes=64)
             c0 = 0
             for i, (width, scalar_cols, gpsimd_cols) in enumerate(LOADS[2 * z + u]):
-                raw = sb.tile([P, 2, width], F32, name="raw%d%d%d" % (z, u, i), tag="raw%d%d%d" % (z, u, i), align_bytes=64)
-                nc.sync.dma_start(raw[:], x_rows[z, u, :, :, c0 : c0 + width])
-                if first_pair:
+                if last_pair:
+                    raw = sb.tile([P, 2, width], F32, name="raw%d%d%d" % (z, u, i), tag="raw%d%d%d" % (z, u, i), align_bytes=64)
+                    nc.sync.dma_start(raw[:], x_rows[z, u, :, :, c0 : c0 + width])
+                    src = raw[:].rearrange("p e t -> p t e")
+                else:
+                    r0 = 0 if i == 0 else T + c0
+                    nc.sync.dma_start(run[:, r0 : T + c0 + width], x_runs[z, u, :, r0 : T + c0 + width])
+                    src = run[:].rearrange("p (e t) -> p t e", e=2)[:, c0 : c0 + width, :]
+                if first_pair and i == len(LOADS[0]) - 1:
                     nc.sync.dma_start(offs_sb[:], offs)
-                src = raw[:].rearrange("p e t -> p t e")
                 if scalar_cols > 0:
                     nc.scalar.copy(window[:, c0 : c0 + scalar_cols, :], src[:, 0:scalar_cols, :])
                 c1 = scalar_cols + gpsimd_cols
@@ -86,8 +95,6 @@ def tile_picked_filmg_silu_e_kernel(tc, xT, w1, w2, w3, offs, cen, pos1, pos2, o
                 if c1 < width:
                     nc.vector.tensor_copy(window[:, c0 + c1 : c0 + width, :], src[:, c1:width, :])
                 c0 += width
-                if i == 0 and after_first_load is not None:
-                    after_first_load()
             words = window[:].rearrange("p t e -> p (t e)").bitcast(U32)
             if first_pair:
                 nc.vector.tensor_copy(picked0[:, :, u, :], words.indirect(offs_sb[:]))
@@ -146,10 +153,6 @@ def tile_picked_filmg_silu_e_kernel(tc, xT, w1, w2, w3, offs, cen, pos1, pos2, o
                 move(on_scalar, res[:, c0:c1], bank[:])
             return res
 
-        def late_quantize():
-            x_codes[0].append(sb.tile([P, HALF], U32, name="xc0b", tag="raw110", align_bytes=64)[:])
-            quantize_x(0, 1, woven0[1], 0, HALF)
-
         load_pair(0, 0)
         load_pair(0, 1)
         woven0 = [sb.tile([P, 4 * HALF], BF16, name="woven0%d" % a, align_bytes=64) for a in range(2)]
@@ -157,8 +160,10 @@ def tile_picked_filmg_silu_e_kernel(tc, xT, w1, w2, w3, offs, cen, pos1, pos2, o
             weave(woven0[a], 0, a, True, 0, QUARTER)
             weave(woven0[a], 0, a, True, QUARTER, HALF)
         quantize_x(0, 0, woven0[0], 0, HALF)
+        x_codes[0].append(sb.tile([P, HALF], U32, name="xc0b", align_bytes=64)[:])
+        quantize_x(0, 1, woven0[1], 0, HALF)
         load_pair(1, 0)
-        load_pair(1, 1, late_quantize)
+        load_pair(1, 1)
 
         raw1 = load_w(after_w1.tile([P, 2, 4, N], F32, name="raw_w1", offset=WOVEN_BYTES // 2, align_bytes=64), w1)
         raw3 = load_w(sb.tile([P, 2, 4, N], F32, name="raw_w3", align_bytes=64), w3)

@@ -40,6 +40,7 @@ def tile_picked_filmg_silu_e_kernel(tc, xT, w1, w2, w3, offs, cen, pos1, pos2, o
         sb = ctx.enter_context(tc.tile_pool(name="sb", bufs=1))
         after_weave = ctx.enter_context(tc.tile_pool(name="after_weave", bufs=1))
         after_w1 = ctx.enter_context(tc.tile_pool(name="after_w1", bufs=1))
+        after_w3 = ctx.enter_context(tc.tile_pool(name="after_w3", bufs=1))
         ps = ctx.enter_context(tc.psum_pool(name="ps", bufs=1))
 
         offs_sb = lists.tile([P, S // PER_COLUMN], U16, name="offs_sb")
@@ -121,11 +122,18 @@ def tile_picked_filmg_silu_e_kernel(tc, xT, w1, w2, w3, offs, cen, pos1, pos2, o
             )
 
         def load_w(raw, w):
-            nc.sync.dma_start(raw[:], w.rearrange("(z p j) n -> p z j n", z=2, p=P, j=4))
+            nc.sync.dma_start(raw, w.rearrange("(z p j) n -> p z j n", z=2, p=P, j=4))
             return raw
 
+        def load_w_pass(raw, w, z):
+            nc.sync.dma_start(raw, w.rearrange("(z p j) n -> z p j n", z=2, p=P, j=4)[z])
+            return raw
+
+        def round_w_pass(rounded, raw):
+            nc.scalar.copy(rounded.rearrange("p (c i) j -> p c j i", i=4), raw.rearrange("p j (c i) -> p c j i", i=4))
+
         def round_w(rounded, raw):
-            nc.scalar.copy(rounded[:].rearrange("p z (c i) j -> p z c j i", i=4), raw[:].rearrange("p z j (c i) -> p z c j i", i=4))
+            nc.scalar.copy(rounded[:].rearrange("p z (c i) j -> p z c j i", i=4), raw.rearrange("p z j (c i) -> p z c j i", i=4))
             return rounded
 
         def quantize_w(name, rounded):
@@ -134,9 +142,8 @@ def tile_picked_filmg_silu_e_kernel(tc, xT, w1, w2, w3, offs, cen, pos1, pos2, o
             nc.vector.quantize_mx(out=codes[:].bitcast(FP8X4), scales=scales[:], in_=rounded[:].rearrange("p z n j -> p (z n j)"))
             return codes, scales
 
-        def product(name, quantized_w, parts, order):
+        def product(name, quantized_w, parts, order, res):
             codes, scales = quantized_w
-            res = sb.tile([P, S], F32, name="res_" + name, align_bytes=64)
             banks = [ps.tile([P, c1 - c0], F32, name="acc_%s%d" % (name, c0)) for c0, c1, on_scalar in parts]
             for z, i in order:
                 c0, c1, on_scalar = parts[i]
@@ -165,37 +172,43 @@ def tile_picked_filmg_silu_e_kernel(tc, xT, w1, w2, w3, offs, cen, pos1, pos2, o
         load_pair(1, 0)
         load_pair(1, 1)
 
-        raw1 = load_w(after_w1.tile([P, 2, 4, N], F32, name="raw_w1", offset=WOVEN_BYTES // 2, align_bytes=64), w1)
-        raw3 = load_w(sb.tile([P, 2, 4, N], F32, name="raw_w3", align_bytes=64), w3)
-        raw2 = load_w(sb.tile([P, 2, 4, N], F32, name="raw_w2", align_bytes=64), w2)
+        raw1a = after_w1.tile([P, 4, N], F32, name="raw_w1a", offset=0, align_bytes=64)
+        raw1b = after_w1.tile([P, 4, N], F32, name="raw_w1b", offset=WOVEN_BYTES, align_bytes=64)
+        raw1 = [load_w_pass(raw1a[:], w1, 0), load_w_pass(raw1b[:], w1, 1)]
+        raw2 = load_w(sb.tile([P, 2, 4, N], F32, name="raw_w2", align_bytes=64)[:], w2)
+        raw3_tile = after_w3.tile([P, 2, 2, 4, N], F32, name="raw_w3", offset=0, align_bytes=64)
+        raw3 = load_w(raw3_tile[:, 0], w3)
         nc.sync.dma_start(cen_sb[:], cen)
         nc.sync.dma_start(pos_sb[0][:], pos1)
         nc.sync.dma_start(pos_sb[1][:], pos2)
-        q1 = quantize_w("w1", round_w(sb.tile([P, 2, N, 4], BF16, name="rounded_w1", align_bytes=64), raw1))
+        rounded1 = sb.tile([P, 2, N, 4], BF16, name="rounded_w1", align_bytes=64)
+        for z in range(2):
+            round_w_pass(rounded1[:, z], raw1[z])
+        q1 = quantize_w("w1", rounded1)
         woven10 = weave(after_w1.tile([P, 4 * HALF], BF16, name="woven10", offset=0, align_bytes=64), 1, 0, True)
         woven11 = weave(after_w1.tile([P, 4 * HALF], BF16, name="woven11", offset=WOVEN_BYTES, align_bytes=64), 1, 1, False)
-        rounded3 = round_w(after_weave.tile([P, 2, N, 4], BF16, name="rounded_w3", offset=0, align_bytes=64), raw3)
+        rounded2 = round_w(sb.tile([P, 2, N, 4], BF16, name="rounded_w2", align_bytes=64), raw2)
         quantize_x(1, 0, woven10, 0, HALF)
         quantize_x(1, 1, woven11, 0, QUARTER)
         quantize_x(1, 1, woven11, QUARTER, HALF)
-        rounded2 = round_w(sb.tile([P, 2, N, 4], BF16, name="rounded_w2", align_bytes=64), raw2)
+        rounded3 = round_w(after_weave.tile([P, 2, N, 4], BF16, name="rounded_w3", offset=0, align_bytes=64), raw3)
         g_parts = [(0, HALF, True), (HALF, HALF + QUARTER, False), (HALF + QUARTER, S, True)]
-        g_sb = product("g", q1, g_parts, [(z, i) for z in range(2) for i in range(len(g_parts))])
-        q3 = quantize_w("w3", rounded3)
+        g_sb = product("g", q1, g_parts, [(z, i) for z in range(2) for i in range(len(g_parts))], sb.tile([P, S], F32, name="res_g", align_bytes=64))
         q2 = quantize_w("w2", rounded2)
+        q3 = quantize_w("w3", rounded3)
         halves = [(0, HALF, True), (HALF, S, True)]
         half_by_half = [(z, i) for i in range(2) for z in range(2)]
-        h_sb = product("h", q3, halves, half_by_half)
-        s_sb = product("s", q2, halves, half_by_half)
+        s_sb = product("s", q2, halves, half_by_half, after_w3.tile([P, S], F32, name="res_s", offset=0, align_bytes=64))
+        h_sb = product("h", q3, halves, half_by_half, after_w3.tile([P, S], F32, name="res_h", offset=4 * S, align_bytes=64))
 
         gc = sb.tile([P, V], F32, name="gc")
         sc = sb.tile([P, V], F32, name="sc")
         nc.vector.tensor_copy(gc[:], g_sb[:].indirect(cen_sb[:]))
+        nc.vector.tensor_copy(sc[:], s_sb[:].indirect(cen_sb[:]))
         prod = sb.tile([P, 2, V], F32, name="prod")
         nc.vector.tensor_tensor(prod[:, 0, :], h_sb[:].indirect(pos_sb[0][:]), gc[:], MULT)
         for v0, v1 in ((0, PIECES[0]), (PIECES[0], V)):
             nc.vector.tensor_tensor(prod[:, 1, v0:v1], h_sb[:].indirect(pos_sb[1][:, v0 // PER_COLUMN : v1 // PER_COLUMN]), gc[:, v0:v1], MULT)
-        nc.vector.tensor_copy(sc[:], s_sb[:].indirect(cen_sb[:]))
 
         acts = []
         v0 = 0

@@ -20,6 +20,7 @@ P = 128
 PER_COLUMN = 16
 HALF = S // 2
 QUARTER = S // 4
+EIGHTH = S // 8
 
 LOADS = [
     [(1024, 352, 0), (1024, 352, 0)],
@@ -38,7 +39,6 @@ def tile_picked_filmg_silu_e_kernel(tc, xT, w1, w2, w3, offs, cen, pos1, pos2, o
     with ExitStack() as ctx:
         lists = ctx.enter_context(tc.tile_pool(name="lists", bufs=1))
         sb = ctx.enter_context(tc.tile_pool(name="sb", bufs=1))
-        after_weave = ctx.enter_context(tc.tile_pool(name="after_weave", bufs=1))
         after_w1 = ctx.enter_context(tc.tile_pool(name="after_w1", bufs=1))
         after_w3 = ctx.enter_context(tc.tile_pool(name="after_w3", bufs=1))
         ps = ctx.enter_context(tc.psum_pool(name="ps", bufs=1))
@@ -55,12 +55,12 @@ def tile_picked_filmg_silu_e_kernel(tc, xT, w1, w2, w3, offs, cen, pos1, pos2, o
         x_rows = xT.rearrange("(z p u e) t -> z u p e t", z=2, p=P, u=2, e=2)
         x_runs = xT.rearrange("(z p u e) t -> z u p (e t)", z=2, p=P, u=2, e=2)
         picked0 = sb.tile([P, 2, 2, HALF], U32, name="picked0")
-        picked1a = after_weave.tile([P, 2, HALF], U32, name="picked1a", offset=0, align_bytes=64)
-        picked1b = sb.tile([P, 2, HALF], U32, name="picked1b")
-        picked = [[picked0[:, 0], picked0[:, 1]], [picked1a[:], picked1b[:]]]
+        picked1a = sb.tile([P, 2, HALF], U32, name="picked1a")
+        picked1b = sb.tile([P, 2 * HALF + QUARTER], U32, name="picked1b", align_bytes=64)
+        picked = [[picked0[:, 0], picked0[:, 1]], [picked1a[:], picked1b[:, 0 : 2 * HALF].rearrange("p (u n) -> p u n", u=2)]]
         x_codes0a = sb.tile([P, HALF], U32, name="xc0a", align_bytes=64)
-        x_codes1a = sb.tile([P, HALF], U32, name="xc1a", align_bytes=64)
-        x_codes1b = after_weave.tile([P, HALF], U32, name="xc1b", offset=W_BF16_BYTES, align_bytes=64)
+        x_codes1a = after_w1.tile([P, HALF], U32, name="xc1a", offset=0, align_bytes=64)
+        x_codes1b = after_w1.tile([P, HALF], U32, name="xc1b", offset=4 * HALF, align_bytes=64)
         x_codes = [[x_codes0a[:]], [x_codes1a[:], x_codes1b[:]]]
         x_scales = [sb.tile([P, S], U8, name="xs%d" % z, align_bytes=64) for z in range(2)]
 
@@ -70,7 +70,7 @@ def tile_picked_filmg_silu_e_kernel(tc, xT, w1, w2, w3, offs, cen, pos1, pos2, o
             else:
                 nc.vector.tensor_copy(dst, src)
 
-        def load_pair(z, u):
+        def load_pair(z, u, before_last_gather=None):
             first_pair = (z, u) == (0, 0)
             window = sb.tile([P, T, 2], BF16, name="window%d%d" % (z, u), tag="raw10" if (z, u) == (1, 1) else "window%d%d" % (z, u), align_bytes=64)
             last_pair = (z, u) == (1, 1)
@@ -99,7 +99,13 @@ def tile_picked_filmg_silu_e_kernel(tc, xT, w1, w2, w3, offs, cen, pos1, pos2, o
             words = window[:].rearrange("p t e -> p (t e)").bitcast(U32)
             if first_pair:
                 nc.vector.tensor_copy(picked0[:, :, u, :], words.indirect(offs_sb[:]))
-            elif (z, u) == (0, 1):
+            elif last_pair:
+                for a, n0, n1 in ((0, 0, QUARTER), (0, QUARTER, HALF), (1, 0, QUARTER), (1, QUARTER, HALF)):
+                    if (a, n0) == (1, QUARTER):
+                        before_last_gather()
+                    c0, c1 = (a * HALF + n0) // PER_COLUMN, (a * HALF + n1) // PER_COLUMN
+                    nc.vector.tensor_copy(picked[z][a][:, u, n0:n1], words.indirect(offs_sb[:, c0:c1]))
+            elif u == 1:
                 cols = QUARTER // PER_COLUMN
                 for q in range(4):
                     n0 = QUARTER * (q % 2)
@@ -125,21 +131,22 @@ def tile_picked_filmg_silu_e_kernel(tc, xT, w1, w2, w3, offs, cen, pos1, pos2, o
             nc.sync.dma_start(raw, w.rearrange("(z p j) n -> p z j n", z=2, p=P, j=4))
             return raw
 
-        def load_w_pass(raw, w, z):
-            nc.sync.dma_start(raw, w.rearrange("(z p j) n -> z p j n", z=2, p=P, j=4)[z])
-            return raw
-
-        def round_w_pass(rounded, raw):
-            nc.scalar.copy(rounded.rearrange("p (c i) j -> p c j i", i=4), raw.rearrange("p j (c i) -> p c j i", i=4))
-
         def round_w(rounded, raw):
             nc.scalar.copy(rounded[:].rearrange("p z (c i) j -> p z c j i", i=4), raw.rearrange("p z j (c i) -> p z c j i", i=4))
             return rounded
 
-        def quantize_w(name, rounded):
-            codes = sb.tile([P, 2 * N], U32, name="codes_" + name, align_bytes=64)
+        def load_w_pass(raw, w, z):
+            nc.sync.dma_start(raw, w.rearrange("(z p j) n -> z p j n", z=2, p=P, j=4)[z])
+            return raw
+
+        def round_w_gpsimd(rounded, raws):
+            for z in range(2):
+                nc.gpsimd.tensor_scalar(rounded[:, z], raws[z].rearrange("p j n -> p n j"), 1.0, 0.0, MULT, ADD)
+            return rounded
+
+        def quantize_w(name, rounded, codes):
             scales = sb.tile([P, 2 * N], U8, name="scales_" + name, align_bytes=64)
-            nc.vector.quantize_mx(out=codes[:].bitcast(FP8X4), scales=scales[:], in_=rounded[:].rearrange("p z n j -> p (z n j)"))
+            nc.vector.quantize_mx(out=codes[:].bitcast(FP8X4), scales=scales[:], in_=rounded.rearrange("p z n j -> p (z n j)"))
             return codes, scales
 
         def product(name, quantized_w, parts, order, res):
@@ -170,36 +177,45 @@ def tile_picked_filmg_silu_e_kernel(tc, xT, w1, w2, w3, offs, cen, pos1, pos2, o
         x_codes[0].append(sb.tile([P, HALF], U32, name="xc0b", align_bytes=64)[:])
         quantize_x(0, 1, woven0[1], 0, HALF)
         load_pair(1, 0)
-        load_pair(1, 1)
+        q1 = []
 
-        raw1a = after_w1.tile([P, 4, N], F32, name="raw_w1a", offset=0, align_bytes=64)
-        raw1b = after_w1.tile([P, 4, N], F32, name="raw_w1b", offset=WOVEN_BYTES, align_bytes=64)
-        raw1 = [load_w_pass(raw1a[:], w1, 0), load_w_pass(raw1b[:], w1, 1)]
+        def prepare_w1():
+            raw1a = sb.tile([P, 4, N], F32, name="raw_w1a", align_bytes=64)
+            raw1b = picked1b[:, HALF + QUARTER : 2 * HALF + QUARTER].bitcast(F32).rearrange("p (j n) -> p j n", j=4)
+            raw1 = [load_w_pass(raw1a[:], w1, 0), load_w_pass(raw1b, w1, 1)]
+            rounded1 = after_w1.tile([P, 3, 2, N, 4], BF16, name="rounded_w1", offset=0, align_bytes=64)
+            round_w_gpsimd(rounded1[:, 0], raw1)
+            q1.extend(quantize_w("w1", rounded1[:, 0], sb.tile([P, 2 * N], U32, name="codes_w1", align_bytes=64)))
+
+        load_pair(1, 1, prepare_w1)
+
         raw2 = load_w(sb.tile([P, 2, 4, N], F32, name="raw_w2", align_bytes=64)[:], w2)
-        raw3_tile = after_w3.tile([P, 2, 2, 4, N], F32, name="raw_w3", offset=0, align_bytes=64)
+        raw3_tile = after_w3.tile([P, 4, 2, 4, N], F32, name="raw_w3", offset=0, align_bytes=64)
         raw3 = load_w(raw3_tile[:, 0], w3)
         nc.sync.dma_start(cen_sb[:], cen)
         nc.sync.dma_start(pos_sb[0][:], pos1)
         nc.sync.dma_start(pos_sb[1][:], pos2)
-        rounded1 = sb.tile([P, 2, N, 4], BF16, name="rounded_w1", align_bytes=64)
-        for z in range(2):
-            round_w_pass(rounded1[:, z], raw1[z])
-        q1 = quantize_w("w1", rounded1)
-        woven10 = weave(after_w1.tile([P, 4 * HALF], BF16, name="woven10", offset=0, align_bytes=64), 1, 0, True)
-        woven11 = weave(after_w1.tile([P, 4 * HALF], BF16, name="woven11", offset=WOVEN_BYTES, align_bytes=64), 1, 1, False)
+        woven10 = sb.tile([P, 4 * HALF], BF16, name="woven10", align_bytes=64)
+        weave(woven10, 1, 0, True, 0, QUARTER)
+        weave(woven10, 1, 0, True, QUARTER, HALF)
         rounded2 = round_w(sb.tile([P, 2, N, 4], BF16, name="rounded_w2", align_bytes=64), raw2)
+        rounded3 = round_w(sb.tile([P, 2, N, 4], BF16, name="rounded_w3", align_bytes=64), raw3)
         quantize_x(1, 0, woven10, 0, HALF)
+        woven11 = after_w1.tile([P, 4 * HALF], BF16, name="woven11", offset=8 * HALF, align_bytes=64)
+        weave(woven11, 1, 1, False, 0, QUARTER)
+        weave(woven11, 1, 1, False, QUARTER, HALF)
         quantize_x(1, 1, woven11, 0, QUARTER)
-        quantize_x(1, 1, woven11, QUARTER, HALF)
-        rounded3 = round_w(after_weave.tile([P, 2, N, 4], BF16, name="rounded_w3", offset=0, align_bytes=64), raw3)
-        g_parts = [(0, HALF, True), (HALF, HALF + QUARTER, False), (HALF + QUARTER, S, True)]
-        g_sb = product("g", q1, g_parts, [(z, i) for z in range(2) for i in range(len(g_parts))], sb.tile([P, S], F32, name="res_g", align_bytes=64))
-        q2 = quantize_w("w2", rounded2)
-        q3 = quantize_w("w3", rounded3)
+        quantize_x(1, 1, woven11, QUARTER, QUARTER + EIGHTH)
+        quantize_x(1, 1, woven11, QUARTER + EIGHTH, HALF)
+        q2 = quantize_w("w2", rounded2[:], sb.tile([P, 2 * N], U32, name="codes_w2", align_bytes=64))
+        g_parts = [(0, HALF, True), (HALF, HALF + QUARTER, False), (HALF + QUARTER, S - EIGHTH, True), (S - EIGHTH, S, True)]
+        g_sb = after_w3.tile([P, S], F32, name="res_g", offset=0, align_bytes=64)
+        product("g", q1, g_parts, [(z, i) for z in range(2) for i in range(len(g_parts))], g_sb)
+        q3 = quantize_w("w3", rounded3[:], after_w3.tile([P, 2 * N], U32, name="codes_w3", offset=12 * S, align_bytes=64))
         halves = [(0, HALF, True), (HALF, S, True)]
         half_by_half = [(z, i) for i in range(2) for z in range(2)]
-        s_sb = product("s", q2, halves, half_by_half, after_w3.tile([P, S], F32, name="res_s", offset=0, align_bytes=64))
-        h_sb = product("h", q3, halves, half_by_half, after_w3.tile([P, S], F32, name="res_h", offset=4 * S, align_bytes=64))
+        s_sb = product("s", q2, halves, half_by_half, after_w3.tile([P, S], F32, name="res_s", offset=4 * S, align_bytes=64))
+        h_sb = product("h", q3, halves, half_by_half, after_w3.tile([P, S], F32, name="res_h", offset=8 * S, align_bytes=64))
 
         gc = sb.tile([P, V], F32, name="gc")
         sc = sb.tile([P, V], F32, name="sc")

@@ -15,23 +15,13 @@ FP8X4 = mybir.dt.float8_e4m3fn_x4
 MULT = mybir.AluOpType.mult
 ADD = mybir.AluOpType.add
 SILU = mybir.ActivationFunctionType.Silu
+COPY = mybir.ActivationFunctionType.Copy
 
 P = 128
 PER_COLUMN = 16
 HALF = S // 2
 QUARTER = S // 4
-EIGHTH = S // 8
-
-LOADS = [
-    [(1024, 352, 0), (1024, 352, 0)],
-    [(640, 320, 320), (896, 320, 0), (512, 128, 0)],
-    [(512, 0, 256), (896, 384, 0), (640, 384, 0)],
-    [(896, 384, 512), (768, 448, 320), (384, 128, 0)],
-]
 PIECES = [192, 192, 128]
-
-WOVEN_BYTES = 4 * HALF * 2
-W_BF16_BYTES = 2 * N * 4 * 2
 
 
 def tile_picked_filmg_silu_e_kernel(tc, xT, w1, w2, w3, offs, cen, pos1, pos2, out):
@@ -39,8 +29,8 @@ def tile_picked_filmg_silu_e_kernel(tc, xT, w1, w2, w3, offs, cen, pos1, pos2, o
     with ExitStack() as ctx:
         lists = ctx.enter_context(tc.tile_pool(name="lists", bufs=1))
         sb = ctx.enter_context(tc.tile_pool(name="sb", bufs=1))
-        after_w1 = ctx.enter_context(tc.tile_pool(name="after_w1", bufs=1))
-        after_w3 = ctx.enter_context(tc.tile_pool(name="after_w3", bufs=1))
+        held = ctx.enter_context(tc.tile_pool(name="held", bufs=1))
+        held2 = ctx.enter_context(tc.tile_pool(name="held2", bufs=1))
         ps = ctx.enter_context(tc.psum_pool(name="ps", bufs=1))
 
         offs_sb = lists.tile([P, S // PER_COLUMN], U16, name="offs_sb")
@@ -52,17 +42,11 @@ def tile_picked_filmg_silu_e_kernel(tc, xT, w1, w2, w3, offs, cen, pos1, pos2, o
         nc.gpsimd.memset(zero_in[:], 0.0)
         nc.scalar.activation(zero[:], zero_in[:], SILU)
 
-        x_rows = xT.rearrange("(z p u e) t -> z u p e t", z=2, p=P, u=2, e=2)
-        x_runs = xT.rearrange("(z p u e) t -> z u p (e t)", z=2, p=P, u=2, e=2)
-        picked0 = sb.tile([P, 2, 2, HALF], U32, name="picked0")
-        picked1a = sb.tile([P, 2, HALF], U32, name="picked1a")
-        picked1b = sb.tile([P, 2 * HALF + QUARTER], U32, name="picked1b", align_bytes=64)
-        picked = [[picked0[:, 0], picked0[:, 1]], [picked1a[:], picked1b[:, 0 : 2 * HALF].rearrange("p (u n) -> p u n", u=2)]]
-        x_codes0a = sb.tile([P, HALF], U32, name="xc0a", align_bytes=64)
-        x_codes1a = after_w1.tile([P, HALF], U32, name="xc1a", offset=0, align_bytes=64)
-        x_codes1b = after_w1.tile([P, HALF], U32, name="xc1b", offset=4 * HALF, align_bytes=64)
-        x_codes = [[x_codes0a[:]], [x_codes1a[:], x_codes1b[:]]]
-        x_scales = [sb.tile([P, S], U8, name="xs%d" % z, align_bytes=64) for z in range(2)]
+        def entries(tile, n0, n1):
+            return tile[:, n0 // PER_COLUMN : n1 // PER_COLUMN]
+
+        def quarter(q):
+            return slice(q * QUARTER, (q + 1) * QUARTER)
 
         def move(on_scalar, dst, src):
             if on_scalar:
@@ -70,176 +54,176 @@ def tile_picked_filmg_silu_e_kernel(tc, xT, w1, w2, w3, offs, cen, pos1, pos2, o
             else:
                 nc.vector.tensor_copy(dst, src)
 
-        def load_pair(z, u, before_last_gather=None):
-            first_pair = (z, u) == (0, 0)
-            window = sb.tile([P, T, 2], BF16, name="window%d%d" % (z, u), tag="raw10" if (z, u) == (1, 1) else "window%d%d" % (z, u), align_bytes=64)
-            last_pair = (z, u) == (1, 1)
-            if not last_pair:
-                run = sb.tile([P, 2 * T], F32, name="raw%d%d" % (z, u), tag="raw%d%d" % (z, u), align_bytes=64)
-            c0 = 0
-            for i, (width, scalar_cols, gpsimd_cols) in enumerate(LOADS[2 * z + u]):
-                if last_pair:
-                    raw = sb.tile([P, 2, width], F32, name="raw%d%d%d" % (z, u, i), tag="raw%d%d%d" % (z, u, i), align_bytes=64)
-                    nc.sync.dma_start(raw[:], x_rows[z, u, :, :, c0 : c0 + width])
-                    src = raw[:].rearrange("p e t -> p t e")
-                else:
-                    r0 = 0 if i == 0 else T + c0
-                    nc.sync.dma_start(run[:, r0 : T + c0 + width], x_runs[z, u, :, r0 : T + c0 + width])
-                    src = run[:].rearrange("p (e t) -> p t e", e=2)[:, c0 : c0 + width, :]
-                if first_pair and i == len(LOADS[0]) - 1:
-                    nc.sync.dma_start(offs_sb[:], offs)
-                if scalar_cols > 0:
-                    nc.scalar.copy(window[:, c0 : c0 + scalar_cols, :], src[:, 0:scalar_cols, :])
-                c1 = scalar_cols + gpsimd_cols
-                if gpsimd_cols > 0:
-                    nc.gpsimd.tensor_scalar(window[:, c0 + scalar_cols : c0 + c1, :], src[:, scalar_cols:c1, :], 1.0, 0.0, MULT, ADD)
-                if c1 < width:
-                    nc.vector.tensor_copy(window[:, c0 + c1 : c0 + width, :], src[:, c1:width, :])
-                c0 += width
-            words = window[:].rearrange("p t e -> p (t e)").bitcast(U32)
-            if first_pair:
-                nc.vector.tensor_copy(picked0[:, :, u, :], words.indirect(offs_sb[:]))
-            elif last_pair:
-                for a, n0, n1 in ((0, 0, QUARTER), (0, QUARTER, HALF), (1, 0, QUARTER), (1, QUARTER, HALF)):
-                    if (a, n0) == (1, QUARTER):
-                        before_last_gather()
-                    c0, c1 = (a * HALF + n0) // PER_COLUMN, (a * HALF + n1) // PER_COLUMN
-                    nc.vector.tensor_copy(picked[z][a][:, u, n0:n1], words.indirect(offs_sb[:, c0:c1]))
-            elif u == 1:
-                cols = QUARTER // PER_COLUMN
-                for q in range(4):
-                    n0 = QUARTER * (q % 2)
-                    nc.vector.tensor_copy(picked[z][q // 2][:, u, n0 : n0 + QUARTER], words.indirect(offs_sb[:, cols * q : cols * (q + 1)]))
-            else:
-                cols = HALF // PER_COLUMN
-                for a in range(2):
-                    nc.vector.tensor_copy(picked[z][a][:, u, :], words.indirect(offs_sb[:, cols * a : cols * (a + 1)]))
-
-        def weave(woven, z, a, on_scalar, n0=0, n1=HALF):
-            dt = U32 if on_scalar else I32
-            move(on_scalar, woven[:, 4 * n0 : 4 * n1].bitcast(dt).rearrange("p (n u) -> p n u", u=2), picked[z][a][:, :, n0:n1].bitcast(dt).rearrange("p u n -> p n u"))
-            return woven
-
-        def quantize_x(z, a, woven, n0, n1):
-            nc.vector.quantize_mx(
-                out=x_codes[z][a][:, n0:n1].bitcast(FP8X4),
-                scales=x_scales[z][:, a * HALF + n0 : a * HALF + n1],
-                in_=woven[:, 4 * n0 : 4 * n1],
-            )
-
-        def load_w(raw, w):
-            nc.sync.dma_start(raw, w.rearrange("(z p j) n -> p z j n", z=2, p=P, j=4))
-            return raw
-
-        def round_w(rounded, raw):
-            nc.scalar.copy(rounded[:].rearrange("p z (c i) j -> p z c j i", i=4), raw.rearrange("p z j (c i) -> p z c j i", i=4))
-            return rounded
-
-        def load_w_pass(raw, w, z):
+        def load_w(raw, w, z):
             nc.sync.dma_start(raw, w.rearrange("(z p j) n -> z p j n", z=2, p=P, j=4)[z])
             return raw
 
-        def round_w_gpsimd(rounded, raws):
-            for z in range(2):
-                nc.gpsimd.tensor_scalar(rounded[:, z], raws[z].rearrange("p j n -> p n j"), 1.0, 0.0, MULT, ADD)
+        def round_w(rounded, raw, on_scalar):
+            move(on_scalar, rounded.rearrange("p (c i) j -> p c j i", i=4), raw.rearrange("p j (c i) -> p c j i", i=4))
             return rounded
 
-        def quantize_w(name, rounded, codes):
-            scales = sb.tile([P, 2 * N], U8, name="scales_" + name, align_bytes=64)
-            nc.vector.quantize_mx(out=codes[:].bitcast(FP8X4), scales=scales[:], in_=rounded.rearrange("p z n j -> p (z n j)"))
+        def raw_tile(name):
+            return sb.tile([P, 4, N], F32, name="raw_" + name, align_bytes=64)[:]
+
+        def rounded_tile(name):
+            return sb.tile([P, N, 4], BF16, name="rounded_" + name, align_bytes=64)[:]
+
+        def quantize_w(name, rounded, codes=None):
+            width = rounded.shape[1]
+            if codes is None:
+                codes = sb.tile([P, width], U32, name="codes_" + name, align_bytes=64)
+            scales = sb.tile([P, width], U8, name="scales_" + name, align_bytes=64)
+            nc.vector.quantize_mx(out=codes[:].bitcast(FP8X4), scales=scales[:], in_=rounded.rearrange("p n j -> p (n j)"))
             return codes, scales
 
-        def product(name, quantized_w, parts, order, res):
-            codes, scales = quantized_w
-            banks = [ps.tile([P, c1 - c0], F32, name="acc_%s%d" % (name, c0)) for c0, c1, on_scalar in parts]
-            for z, i in order:
-                c0, c1, on_scalar = parts[i]
-                nc.tensor.matmul_mx(
-                    out=banks[i][:],
-                    lhsT=codes[:, z * N : (z + 1) * N].bitcast(FP8X4),
-                    lhsT_scale=scales[:, z * N : (z + 1) * N],
-                    rhs=x_codes[z][c0 // HALF][:, c0 % HALF : c0 % HALF + c1 - c0].bitcast(FP8X4),
-                    rhs_scale=x_scales[z][:, c0:c1],
-                    start=(z == 0),
-                    stop=(z == 1),
-                )
-            for bank, (c0, c1, on_scalar) in zip(banks, parts):
-                move(on_scalar, res[:, c0:c1], bank[:])
-            return res
+        x_planes = xT.rearrange("(z p j) t -> z j p t", z=2, p=P, j=4)
+        woven = [[sb.tile([P, QUARTER, 4], BF16, name="woven%d%d" % (z, q), align_bytes=64) for q in range(4)] for z in range(2)]
+        picked = [sb.tile([P, 4, S], BF16, name="picked%d" % z, align_bytes=64) for z in range(2)]
+        x_codes = [sb.tile([P, S], U32, name="xc0", align_bytes=64)]
+        x_scales = [sb.tile([P, S], U8, name="xs%d" % z, align_bytes=64) for z in range(2)]
 
-        load_pair(0, 0)
-        load_pair(0, 1)
-        woven0 = [sb.tile([P, 4 * HALF], BF16, name="woven0%d" % a, align_bytes=64) for a in range(2)]
-        for a in range(2):
-            weave(woven0[a], 0, a, True, 0, QUARTER)
-            weave(woven0[a], 0, a, True, QUARTER, HALF)
-        quantize_x(0, 0, woven0[0], 0, HALF)
-        x_codes[0].append(sb.tile([P, HALF], U32, name="xc0b", align_bytes=64)[:])
-        quantize_x(0, 1, woven0[1], 0, HALF)
-        load_pair(1, 0)
-        q1 = []
+        def load_plane(z, j):
+            plane = sb.tile([P, T], F32, name="plane%d%d" % (z, j), align_bytes=64)
+            nc.sync.dma_start(plane[:], x_planes[z, j])
+            if (z, j) == (0, 0):
+                nc.sync.dma_start(offs_sb[:], offs)
+            return plane
 
-        def prepare_w1():
-            raw1a = sb.tile([P, 4, N], F32, name="raw_w1a", align_bytes=64)
-            raw1b = picked1b[:, HALF + QUARTER : 2 * HALF + QUARTER].bitcast(F32).rearrange("p (j n) -> p j n", j=4)
-            raw1 = [load_w_pass(raw1a[:], w1, 0), load_w_pass(raw1b, w1, 1)]
-            rounded1 = after_w1.tile([P, 3, 2, N, 4], BF16, name="rounded_w1", offset=0, align_bytes=64)
-            round_w_gpsimd(rounded1[:, 0], raw1)
-            q1.extend(quantize_w("w1", rounded1[:, 0], sb.tile([P, 2 * N], U32, name="codes_w1", align_bytes=64)))
+        def gather_plane(z, j, on_vector, cuts):
+            plane = load_plane(z, j)
+            for q in range(on_vector):
+                nc.vector.tensor_copy(woven[z][q][:, :, j], plane[:].indirect(entries(offs_sb, q * QUARTER, (q + 1) * QUARTER)))
+            for n0, n1 in cuts:
+                nc.scalar.activation(picked[z][:, j, n0:n1], plane[:].indirect(entries(offs_sb, n0, n1)), COPY)
 
-        load_pair(1, 1, prepare_w1)
+        def weave(z, q, j0, j1, on_scalar=False):
+            src = picked[z][:, j0:j1, quarter(q)]
+            if j1 - j0 == 4:
+                move(on_scalar, woven[z][q][:].rearrange("p (c i) j -> p c j i", i=4), src.rearrange("p j (c i) -> p c j i", i=4))
+            else:
+                move(on_scalar, woven[z][q][:, :, j0:j1], src.rearrange("p j n -> p n j"))
 
-        raw2 = load_w(sb.tile([P, 2, 4, N], F32, name="raw_w2", align_bytes=64)[:], w2)
-        raw3_tile = after_w3.tile([P, 4, 2, 4, N], F32, name="raw_w3", offset=0, align_bytes=64)
-        raw3 = load_w(raw3_tile[:, 0], w3)
+        def quantize_x(z, q):
+            nc.vector.quantize_mx(out=x_codes[z][:, quarter(q)].bitcast(FP8X4), scales=x_scales[z][:, quarter(q)], in_=woven[z][q][:].rearrange("p n j -> p (n j)"))
+
+        for j in range(4):
+            gather_plane(0, j, 1, [(QUARTER, S)])
+        for q in range(1, 4):
+            weave(0, q, 0, 4)
+            quantize_x(0, q - 1)
+        quantize_x(0, 3)
+        for j in range(2):
+            gather_plane(1, j, 1, [(QUARTER, S)])
+        for q in range(1, 4):
+            weave(1, q, 0, 2)
+        gather_plane(1, 2, 2, [(HALF, S)])
+        raw10 = load_w(raw_tile("w10"), w1, 0)
+        raw30 = load_w(raw_tile("w30"), w3, 0)
+        q10 = quantize_w("w10", round_w(rounded_tile("w10"), raw10, True))
+        q30 = quantize_w("w30", round_w(rounded_tile("w30"), raw30, True))
+        gather_plane(1, 3, 2, [(3 * QUARTER, S), (HALF, 3 * QUARTER)])
+        raw11 = load_w(held.tile([P, 4, N], F32, name="raw_w11", offset=3584, align_bytes=64)[:], w1, 1)
+        raw31 = load_w(raw_tile("w31"), w3, 1)
+        raw20 = load_w(held2.tile([P, 4, N], F32, name="raw_w20", offset=3072, align_bytes=64)[:], w2, 0)
+        raw21 = load_w(raw_tile("w21"), w2, 1)
         nc.sync.dma_start(cen_sb[:], cen)
         nc.sync.dma_start(pos_sb[0][:], pos1)
         nc.sync.dma_start(pos_sb[1][:], pos2)
-        woven10 = sb.tile([P, 4 * HALF], BF16, name="woven10", align_bytes=64)
-        weave(woven10, 1, 0, True, 0, QUARTER)
-        weave(woven10, 1, 0, True, QUARTER, HALF)
-        rounded2 = round_w(sb.tile([P, 2, N, 4], BF16, name="rounded_w2", align_bytes=64), raw2)
-        rounded3 = round_w(sb.tile([P, 2, N, 4], BF16, name="rounded_w3", align_bytes=64), raw3)
-        quantize_x(1, 0, woven10, 0, HALF)
-        woven11 = after_w1.tile([P, 4 * HALF], BF16, name="woven11", offset=8 * HALF, align_bytes=64)
-        weave(woven11, 1, 1, False, 0, QUARTER)
-        weave(woven11, 1, 1, False, QUARTER, HALF)
-        quantize_x(1, 1, woven11, 0, QUARTER)
-        quantize_x(1, 1, woven11, QUARTER, QUARTER + EIGHTH)
-        quantize_x(1, 1, woven11, QUARTER + EIGHTH, HALF)
-        q2 = quantize_w("w2", rounded2[:], sb.tile([P, 2 * N], U32, name="codes_w2", align_bytes=64))
-        g_parts = [(0, HALF, True), (HALF, HALF + QUARTER, False), (HALF + QUARTER, S - EIGHTH, True), (S - EIGHTH, S, True)]
-        g_sb = after_w3.tile([P, S], F32, name="res_g", offset=0, align_bytes=64)
-        product("g", q1, g_parts, [(z, i) for z in range(2) for i in range(len(g_parts))], g_sb)
-        q3 = quantize_w("w3", rounded3[:], after_w3.tile([P, 2 * N], U32, name="codes_w3", offset=12 * S, align_bytes=64))
-        halves = [(0, HALF, True), (HALF, S, True)]
-        half_by_half = [(z, i) for i in range(2) for z in range(2)]
-        s_sb = product("s", q2, halves, half_by_half, after_w3.tile([P, S], F32, name="res_s", offset=4 * S, align_bytes=64))
-        h_sb = product("h", q3, halves, half_by_half, after_w3.tile([P, S], F32, name="res_h", offset=8 * S, align_bytes=64))
+        rounded11 = rounded_tile("w11")
+        nc.gpsimd.tensor_scalar(rounded11, raw11.rearrange("p j n -> p n j"), 1.0, 0.0, MULT, ADD)
+        weave(1, 3, 2, 4, True)
+        rounded31 = round_w(rounded_tile("w31"), raw31, True)
+        rounded2 = held.tile([P, 2, N, 4], BF16, name="rounded_w2", offset=5120, align_bytes=64)
+        round_w(rounded2[:, 0], raw20, True)
+        weave(1, 2, 2, 4)
+        q11 = quantize_w("w11", rounded11, sb.tile([P, N], U32, name="codes_w11", tag="codes_late", align_bytes=64))
+        x_codes.append(held.tile([P, S], U32, name="xc1", offset=0, align_bytes=64))
+        quantize_x(1, 0)
+        quantize_x(1, 1)
+        quantize_x(1, 2)
+        q31 = quantize_w("w31", rounded31, held.tile([P, N], U32, name="codes_w31", offset=4096, align_bytes=64))
+        quantize_x(1, 3)
+        round_w(rounded2[:, 1], raw21, False)
 
+        def one_pass(bank, quantized_w, w0, z, n0, n1, start, stop):
+            codes, scales = quantized_w
+            nc.tensor.matmul_mx(
+                out=bank,
+                lhsT=codes[:, w0 : w0 + N].bitcast(FP8X4),
+                lhsT_scale=scales[:, w0 : w0 + N],
+                rhs=x_codes[z][:, n0:n1].bitcast(FP8X4),
+                rhs_scale=x_scales[z][:, n0:n1],
+                start=start,
+                stop=stop,
+            )
+
+        g_parts = [(0, HALF), (HALF, 3 * QUARTER), (3 * QUARTER, S)]
+        h_parts = [(0, HALF), (HALF, S)]
+        g_banks = [ps.tile([P, n1 - n0], F32, name="acc_g%d" % n0) for n0, n1 in g_parts]
+        h_banks = [ps.tile([P, n1 - n0], F32, name="acc_h%d" % n0) for n0, n1 in h_parts]
+        for banks, parts, quantized_w in ((g_banks, g_parts, q10), (h_banks, h_parts, q30)):
+            for i, (n0, n1) in enumerate(parts):
+                one_pass(banks[i][:], quantized_w, 0, 0, n0, n1, True, False)
+
+        def g_pass(q):
+            bank = g_banks[0][:, quarter(q)] if q < 2 else g_banks[q - 1][:]
+            one_pass(bank, q11, 0, 1, q * QUARTER, (q + 1) * QUARTER, False, q > 0)
+
+        for q in range(3):
+            g_pass(q)
+        one_pass(h_banks[0][:], q31, 0, 1, 0, HALF, False, True)
+        g_pass(3)
+        one_pass(h_banks[1][:], q31, 0, 1, HALF, S, False, True)
+        g_sb = held2.tile([P, S], F32, name="res_g", offset=0, align_bytes=64)
+        h_sb = held2.tile([P, S], F32, name="res_h", offset=4096, align_bytes=64)
+        s_sb = sb.tile([P, S], F32, name="res_s", align_bytes=64)
+        for i, (n0, n1) in enumerate(g_parts):
+            move(i < 2, g_sb[:, n0:n1], g_banks[i][:])
+        q2 = [quantize_w("w20", rounded2[:, 0], sb.tile([P, N], U32, name="codes_w20", tag="codes_late", align_bytes=64))]
+        for i, (n0, n1) in enumerate(h_parts):
+            move(i < 1, h_sb[:, n0:n1], h_banks[i][:])
+        q2.append(quantize_w("w21", rounded2[:, 1], held.tile([P, N], U32, name="codes_w21", offset=4096, align_bytes=64)))
+
+        bounds = [sum(PIECES[:i]) for i in range(len(PIECES) + 1)]
+        pieces = list(zip(bounds[:-1], bounds[1:]))
         gc = sb.tile([P, V], F32, name="gc")
-        sc = sb.tile([P, V], F32, name="sc")
-        nc.vector.tensor_copy(gc[:], g_sb[:].indirect(cen_sb[:]))
-        nc.vector.tensor_copy(sc[:], s_sb[:].indirect(cen_sb[:]))
-        prod = sb.tile([P, 2, V], F32, name="prod")
-        nc.vector.tensor_tensor(prod[:, 0, :], h_sb[:].indirect(pos_sb[0][:]), gc[:], MULT)
         for v0, v1 in ((0, PIECES[0]), (PIECES[0], V)):
-            nc.vector.tensor_tensor(prod[:, 1, v0:v1], h_sb[:].indirect(pos_sb[1][:, v0 // PER_COLUMN : v1 // PER_COLUMN]), gc[:, v0:v1], MULT)
+            nc.scalar.activation(gc[:, v0:v1], g_sb[:].indirect(entries(cen_sb, v0, v1)), COPY)
+        s_banks = [ps.tile([P, HALF], F32, name="acc_s%d" % a) for a in range(2)]
+        for z in range(2):
+            for a in range(2):
+                one_pass(s_banks[a][:], q2[z], 0, z, a * HALF, (a + 1) * HALF, z == 0, z == 1)
+        for a in range(2):
+            nc.scalar.copy(s_sb[:, a * HALF : (a + 1) * HALF], s_banks[a][:])
 
+        sc = sb.tile([P, V], F32, name="sc")
+        prod = sb.tile([P, 2, V], F32, name="prod")
+        for v0, v1 in pieces:
+            nc.scalar.activation(sc[:, v0:v1], s_sb[:].indirect(entries(cen_sb, v0, v1)), COPY)
         acts = []
-        v0 = 0
-        for i, width in enumerate(PIECES):
-            cols = slice(v0, v0 + width)
-            pre = sb.tile([P, 2, width], F32, name="pre%d" % i)
-            act = sb.tile([P, 2, width], F32, name="act%d" % i)
-            nc.vector.tensor_tensor(pre[:], prod[:, :, cols], sc[:, cols].unsqueeze(1).to_broadcast([P, 2, width]), ADD)
+
+        def neighbours(v0, v1):
+            for d in range(2):
+                nc.vector.tensor_tensor(prod[:, d, v0:v1], h_sb[:].indirect(entries(pos_sb[d], v0, v1)), gc[:, v0:v1], MULT)
+
+        def shift(i):
+            v0, v1 = pieces[i]
+            pre = sb.tile([P, 2, v1 - v0], F32, name="pre%d" % i)
+            act = sb.tile([P, 2, v1 - v0], F32, name="act%d" % i)
+            nc.vector.tensor_tensor(pre[:], prod[:, :, v0:v1], sc[:, v0:v1].unsqueeze(1).to_broadcast([P, 2, v1 - v0]), ADD)
             nc.scalar.activation(act[:], pre[:], SILU, bias=zero[:])
             acts.append(act)
-            v0 += width
-        v0 = 0
-        for i, width in enumerate(PIECES):
-            cols = slice(v0, v0 + width)
-            total = sb.tile([P, width], F32, name="total%d" % i)
+
+        def finish(i):
+            v0, v1 = pieces[i]
+            total = sb.tile([P, v1 - v0], F32, name="total%d" % i)
             nc.vector.tensor_tensor(total[:], acts[i][:, 0, :], acts[i][:, 1, :], ADD)
-            nc.sync.dma_start(out[:, cols], total[:])
-            v0 += width
+            nc.sync.dma_start(out[:, v0:v1], total[:])
+
+        neighbours(0, PIECES[0])
+        neighbours(PIECES[0], V)
+        shift(0)
+        shift(1)
+        shift(2)
+        for i in range(3):
+            finish(i)

@@ -7,7 +7,6 @@ FLOPS = 3 * 2 * K * S * N
 
 F32 = mybir.dt.float32
 BF16 = mybir.dt.bfloat16
-I32 = mybir.dt.int32
 U32 = mybir.dt.uint32
 U16 = mybir.dt.uint16
 U8 = mybir.dt.uint8
@@ -22,6 +21,7 @@ PER_COLUMN = 16
 HALF = S // 2
 QUARTER = S // 4
 PIECES = [192, 192, 128]
+HEAD = 1152
 
 
 def tile_picked_filmg_silu_e_kernel(tc, xT, w1, w2, w3, offs, cen, pos1, pos2, out):
@@ -29,8 +29,8 @@ def tile_picked_filmg_silu_e_kernel(tc, xT, w1, w2, w3, offs, cen, pos1, pos2, o
     with ExitStack() as ctx:
         lists = ctx.enter_context(tc.tile_pool(name="lists", bufs=1))
         sb = ctx.enter_context(tc.tile_pool(name="sb", bufs=1))
-        held = ctx.enter_context(tc.tile_pool(name="held", bufs=1))
-        held2 = ctx.enter_context(tc.tile_pool(name="held2", bufs=1))
+        shared = ctx.enter_context(tc.tile_pool(name="shared", bufs=1))
+        results = ctx.enter_context(tc.tile_pool(name="results", bufs=1))
         ps = ctx.enter_context(tc.psum_pool(name="ps", bufs=1))
 
         offs_sb = lists.tile([P, S // PER_COLUMN], U16, name="offs_sb")
@@ -48,159 +48,157 @@ def tile_picked_filmg_silu_e_kernel(tc, xT, w1, w2, w3, offs, cen, pos1, pos2, o
         def quarter(q):
             return slice(q * QUARTER, (q + 1) * QUARTER)
 
-        def move(on_scalar, dst, src):
-            if on_scalar:
-                nc.scalar.copy(dst, src)
-            else:
-                nc.vector.tensor_copy(dst, src)
-
-        def load_w(raw, w, z):
-            nc.sync.dma_start(raw, w.rearrange("(z p j) n -> z p j n", z=2, p=P, j=4)[z])
-            return raw
-
-        def round_w(rounded, raw, on_scalar):
-            move(on_scalar, rounded.rearrange("p (c i) j -> p c j i", i=4), raw.rearrange("p j (c i) -> p c j i", i=4))
-            return rounded
-
-        def raw_tile(name):
-            return sb.tile([P, 4, N], F32, name="raw_" + name, align_bytes=64)[:]
-
-        def rounded_tile(name):
-            return sb.tile([P, N, 4], BF16, name="rounded_" + name, align_bytes=64)[:]
-
-        def quantize_w(name, rounded, codes=None):
-            width = rounded.shape[1]
-            if codes is None:
-                codes = sb.tile([P, width], U32, name="codes_" + name, align_bytes=64)
-            scales = sb.tile([P, width], U8, name="scales_" + name, align_bytes=64)
-            nc.vector.quantize_mx(out=codes[:].bitcast(FP8X4), scales=scales[:], in_=rounded.rearrange("p n j -> p (n j)"))
-            return codes, scales
+        def half(a):
+            return slice(a * HALF, (a + 1) * HALF)
 
         x_planes = xT.rearrange("(z p j) t -> z j p t", z=2, p=P, j=4)
         woven = [[sb.tile([P, QUARTER, 4], BF16, name="woven%d%d" % (z, q), align_bytes=64) for q in range(4)] for z in range(2)]
         picked = [sb.tile([P, 4, S], BF16, name="picked%d" % z, align_bytes=64) for z in range(2)]
-        x_codes = [sb.tile([P, S], U32, name="xc0", align_bytes=64)]
-        x_scales = [sb.tile([P, S], U8, name="xs%d" % z, align_bytes=64) for z in range(2)]
+        x_codes = [sb.tile([P, S], U32, name="x_codes0", align_bytes=64)]
+        x_scales = [sb.tile([P, S], U8, name="x_scales%d" % z, align_bytes=64) for z in range(2)]
+
+        def plane_tile(z, j):
+            return sb.tile([P, T], F32, name="plane%d%d" % (z, j), align_bytes=64)
 
         def load_plane(z, j):
-            plane = sb.tile([P, T], F32, name="plane%d%d" % (z, j), align_bytes=64)
+            plane = plane_tile(z, j)
             nc.sync.dma_start(plane[:], x_planes[z, j])
             if (z, j) == (0, 0):
                 nc.sync.dma_start(offs_sb[:], offs)
             return plane
 
-        def gather_plane(z, j, on_vector, cuts):
-            plane = load_plane(z, j)
+        def gather_plane(plane, z, j, on_vector, cuts):
             for q in range(on_vector):
                 nc.vector.tensor_copy(woven[z][q][:, :, j], plane[:].indirect(entries(offs_sb, q * QUARTER, (q + 1) * QUARTER)))
             for n0, n1 in cuts:
                 nc.scalar.activation(picked[z][:, j, n0:n1], plane[:].indirect(entries(offs_sb, n0, n1)), COPY)
 
-        def weave(z, q, j0, j1, on_scalar=False):
-            src = picked[z][:, j0:j1, quarter(q)]
-            if j1 - j0 == 4:
-                move(on_scalar, woven[z][q][:].rearrange("p (c i) j -> p c j i", i=4), src.rearrange("p j (c i) -> p c j i", i=4))
-            else:
-                move(on_scalar, woven[z][q][:, :, j0:j1], src.rearrange("p j n -> p n j"))
+        def weave_all(z, q):
+            nc.vector.tensor_copy(
+                woven[z][q][:].rearrange("p (c i) j -> p c j i", i=4),
+                picked[z][:, :, quarter(q)].rearrange("p j (c i) -> p c j i", i=4),
+            )
+
+        def weave_two(copy, z, q, j0):
+            copy(woven[z][q][:, :, j0 : j0 + 2], picked[z][:, j0 : j0 + 2, quarter(q)].rearrange("p j n -> p n j"))
 
         def quantize_x(z, q):
             nc.vector.quantize_mx(out=x_codes[z][:, quarter(q)].bitcast(FP8X4), scales=x_scales[z][:, quarter(q)], in_=woven[z][q][:].rearrange("p n j -> p (n j)"))
 
+        def load_w(raw, w, z):
+            nc.sync.dma_start(raw[:], w.rearrange("(z p j) n -> z p j n", z=2, p=P, j=4)[z])
+            return raw
+
+        def raw_tile(name):
+            return sb.tile([P, 4, N], F32, name="raw_" + name, align_bytes=64)
+
+        def rounded_tile(name, passes):
+            return sb.tile([P, passes * N, 4], BF16, name="rounded_" + name, align_bytes=64)
+
+        def round_w(copy, rounded, at, raw):
+            copy(rounded[:, at * N : (at + 1) * N].rearrange("p (c i) j -> p c j i", i=4), raw[:].rearrange("p j (c i) -> p c j i", i=4))
+
+        def codes_tile(name, passes):
+            return sb.tile([P, passes * N], U32, name="codes_" + name, align_bytes=64)
+
+        def quantize_w(name, codes, rounded):
+            width = rounded.shape[1]
+            scales = sb.tile([P, width], U8, name="scales_" + name, align_bytes=64)
+            nc.vector.quantize_mx(out=codes[:].bitcast(FP8X4), scales=scales[:], in_=rounded[:].rearrange("p n j -> p (n j)"))
+            return [(codes[:, n0 : n0 + N], scales[:, n0 : n0 + N]) for n0 in range(0, width, N)]
+
+        def one_pass(bank, a, quantized_w, z):
+            codes, scales = quantized_w
+            nc.tensor.matmul_mx(
+                out=bank[:],
+                lhsT=codes.bitcast(FP8X4),
+                lhsT_scale=scales,
+                rhs=x_codes[z][:, half(a)].bitcast(FP8X4),
+                rhs_scale=x_scales[z][:, half(a)],
+                start=z == 0,
+                stop=z == 1,
+            )
+
         for j in range(4):
-            gather_plane(0, j, 1, [(QUARTER, S)])
+            gather_plane(load_plane(0, j), 0, j, 1, [(QUARTER, S)])
         for q in range(1, 4):
-            weave(0, q, 0, 4)
+            weave_all(0, q)
             quantize_x(0, q - 1)
         quantize_x(0, 3)
         for j in range(2):
-            gather_plane(1, j, 1, [(QUARTER, S)])
+            gather_plane(load_plane(1, j), 1, j, 1, [(QUARTER, S)])
         for q in range(1, 4):
-            weave(1, q, 0, 2)
-        gather_plane(1, 2, 2, [(HALF, S)])
+            weave_two(nc.vector.tensor_copy, 1, q, 0)
+        gather_plane(load_plane(1, 2), 1, 2, 2, [(HALF, S)])
+
+        last = plane_tile(1, 3)
+        nc.sync.dma_start(last[:, :HEAD], x_planes[1, 3][:, :HEAD])
         raw10 = load_w(raw_tile("w10"), w1, 0)
-        raw30 = load_w(raw_tile("w30"), w3, 0)
-        q10 = quantize_w("w10", round_w(rounded_tile("w10"), raw10, True))
-        q30 = quantize_w("w30", round_w(rounded_tile("w30"), raw30, True))
-        gather_plane(1, 3, 2, [(3 * QUARTER, S), (HALF, 3 * QUARTER)])
-        raw11 = load_w(held.tile([P, 4, N], F32, name="raw_w11", offset=3584, align_bytes=64)[:], w1, 1)
+        nc.sync.dma_start(last[:, HEAD:], x_planes[1, 3][:, HEAD:])
+        rounded10 = rounded_tile("w10", 1)
+        round_w(nc.scalar.copy, rounded10, 0, raw10)
+        q1 = quantize_w("w10", codes_tile("w10", 1), rounded10)
+        gather_plane(last, 1, 3, 2, [(HALF, 3 * QUARTER), (3 * QUARTER, S)])
+
+        raw30 = load_w(shared.tile([P, 4, N], F32, name="raw_w30", offset=3584, align_bytes=64), w3, 0)
+        raw11 = load_w(raw_tile("w11"), w1, 1)
         raw31 = load_w(raw_tile("w31"), w3, 1)
-        raw20 = load_w(held2.tile([P, 4, N], F32, name="raw_w20", offset=3072, align_bytes=64)[:], w2, 0)
+        raw20 = load_w(results.tile([P, 4, N], F32, name="raw_w20", offset=0, align_bytes=64), w2, 0)
         raw21 = load_w(raw_tile("w21"), w2, 1)
         nc.sync.dma_start(cen_sb[:], cen)
         nc.sync.dma_start(pos_sb[0][:], pos1)
         nc.sync.dma_start(pos_sb[1][:], pos2)
-        rounded11 = rounded_tile("w11")
-        nc.gpsimd.tensor_scalar(rounded11, raw11.rearrange("p j n -> p n j"), 1.0, 0.0, MULT, ADD)
-        weave(1, 3, 2, 4, True)
-        rounded31 = round_w(rounded_tile("w31"), raw31, True)
-        rounded2 = held.tile([P, 2, N, 4], BF16, name="rounded_w2", offset=5120, align_bytes=64)
-        round_w(rounded2[:, 0], raw20, True)
-        weave(1, 2, 2, 4)
-        q11 = quantize_w("w11", rounded11, sb.tile([P, N], U32, name="codes_w11", tag="codes_late", align_bytes=64))
-        x_codes.append(held.tile([P, S], U32, name="xc1", offset=0, align_bytes=64))
+
+        rounded11 = rounded_tile("w11", 1)
+        rounded30 = rounded_tile("w30", 1)
+        rounded31 = rounded_tile("w31", 1)
+        rounded2 = rounded_tile("w2", 2)
+        nc.gpsimd.tensor_scalar(rounded30[:], raw30[:].rearrange("p j n -> p n j"), 1.0, 0.0, MULT, ADD)
+        weave_two(nc.scalar.copy, 1, 2, 2)
+        weave_two(nc.scalar.copy, 1, 3, 2)
+        round_w(nc.scalar.copy, rounded31, 0, raw31)
+        round_w(nc.scalar.copy, rounded2, 0, raw20)
+
+        q3 = quantize_w("w30", codes_tile("w30", 1), rounded30)
+        x_codes.append(shared.tile([P, S], U32, name="x_codes1", offset=0, align_bytes=64))
         quantize_x(1, 0)
+        round_w(nc.vector.tensor_copy, rounded11, 0, raw11)
         quantize_x(1, 1)
+        q1 = q1 + quantize_w("w11", results.tile([P, N], U32, name="codes_w11", offset=4096, align_bytes=64), rounded11)
         quantize_x(1, 2)
-        q31 = quantize_w("w31", rounded31, held.tile([P, N], U32, name="codes_w31", offset=4096, align_bytes=64))
         quantize_x(1, 3)
-        round_w(rounded2[:, 1], raw21, False)
+        q3 = q3 + quantize_w("w31", codes_tile("w31", 1), rounded31)
+        round_w(nc.vector.tensor_copy, rounded2, 1, raw21)
 
-        def one_pass(bank, quantized_w, w0, z, n0, n1, start, stop):
-            codes, scales = quantized_w
-            nc.tensor.matmul_mx(
-                out=bank,
-                lhsT=codes[:, w0 : w0 + N].bitcast(FP8X4),
-                lhsT_scale=scales[:, w0 : w0 + N],
-                rhs=x_codes[z][:, n0:n1].bitcast(FP8X4),
-                rhs_scale=x_scales[z][:, n0:n1],
-                start=start,
-                stop=stop,
-            )
+        g_banks = [ps.tile([P, HALF], F32, name="acc_g%d" % a) for a in range(2)]
+        h_banks = [ps.tile([P, HALF], F32, name="acc_h%d" % a) for a in range(2)]
+        s_banks = [ps.tile([P, HALF], F32, name="acc_s%d" % a) for a in range(2)]
+        for z in range(2):
+            for banks, both in ((g_banks, q1), (h_banks, q3)):
+                for a in range(2):
+                    one_pass(banks[a], a, both[z], z)
 
-        g_parts = [(0, HALF), (HALF, 3 * QUARTER), (3 * QUARTER, S)]
-        h_parts = [(0, HALF), (HALF, S)]
-        g_banks = [ps.tile([P, n1 - n0], F32, name="acc_g%d" % n0) for n0, n1 in g_parts]
-        h_banks = [ps.tile([P, n1 - n0], F32, name="acc_h%d" % n0) for n0, n1 in h_parts]
-        for banks, parts, quantized_w in ((g_banks, g_parts, q10), (h_banks, h_parts, q30)):
-            for i, (n0, n1) in enumerate(parts):
-                one_pass(banks[i][:], quantized_w, 0, 0, n0, n1, True, False)
-
-        def g_pass(q):
-            bank = g_banks[0][:, quarter(q)] if q < 2 else g_banks[q - 1][:]
-            one_pass(bank, q11, 0, 1, q * QUARTER, (q + 1) * QUARTER, False, q > 0)
-
-        for q in range(3):
-            g_pass(q)
-        one_pass(h_banks[0][:], q31, 0, 1, 0, HALF, False, True)
-        g_pass(3)
-        one_pass(h_banks[1][:], q31, 0, 1, HALF, S, False, True)
-        g_sb = held2.tile([P, S], F32, name="res_g", offset=0, align_bytes=64)
-        h_sb = held2.tile([P, S], F32, name="res_h", offset=4096, align_bytes=64)
+        g_sb = results.tile([P, S], F32, name="res_g", offset=0, align_bytes=64)
+        h_sb = sb.tile([P, S], F32, name="res_h", align_bytes=64)
         s_sb = sb.tile([P, S], F32, name="res_s", align_bytes=64)
-        for i, (n0, n1) in enumerate(g_parts):
-            move(i < 2, g_sb[:, n0:n1], g_banks[i][:])
-        q2 = [quantize_w("w20", rounded2[:, 0], sb.tile([P, N], U32, name="codes_w20", tag="codes_late", align_bytes=64))]
-        for i, (n0, n1) in enumerate(h_parts):
-            move(i < 1, h_sb[:, n0:n1], h_banks[i][:])
-        q2.append(quantize_w("w21", rounded2[:, 1], held.tile([P, N], U32, name="codes_w21", offset=4096, align_bytes=64)))
+        nc.scalar.copy(g_sb[:, half(0)], g_banks[0][:])
+        nc.vector.tensor_copy(g_sb[:, half(1)], g_banks[1][:])
+        q2 = quantize_w("w2", results.tile([P, 2 * N], U32, name="codes_w2", offset=4096, align_bytes=64), rounded2)
+        for a in range(2):
+            for z in range(2):
+                one_pass(s_banks[a], a, q2[z], z)
+        nc.scalar.copy(h_sb[:, half(0)], h_banks[0][:])
+        nc.vector.tensor_copy(h_sb[:, half(1)], h_banks[1][:])
 
         bounds = [sum(PIECES[:i]) for i in range(len(PIECES) + 1)]
         pieces = list(zip(bounds[:-1], bounds[1:]))
         gc = sb.tile([P, V], F32, name="gc")
-        for v0, v1 in ((0, PIECES[0]), (PIECES[0], V)):
-            nc.scalar.activation(gc[:, v0:v1], g_sb[:].indirect(entries(cen_sb, v0, v1)), COPY)
-        s_banks = [ps.tile([P, HALF], F32, name="acc_s%d" % a) for a in range(2)]
-        for z in range(2):
-            for a in range(2):
-                one_pass(s_banks[a][:], q2[z], 0, z, a * HALF, (a + 1) * HALF, z == 0, z == 1)
-        for a in range(2):
-            nc.scalar.copy(s_sb[:, a * HALF : (a + 1) * HALF], s_banks[a][:])
-
         sc = sb.tile([P, V], F32, name="sc")
         prod = sb.tile([P, 2, V], F32, name="prod")
-        for v0, v1 in pieces:
-            nc.scalar.activation(sc[:, v0:v1], s_sb[:].indirect(entries(cen_sb, v0, v1)), COPY)
         acts = []
+
+        def centre(dst, src, v0, v1):
+            nc.scalar.activation(dst[:, v0:v1], src[:].indirect(entries(cen_sb, v0, v1)), COPY)
 
         def neighbours(v0, v1):
             for d in range(2):
@@ -220,10 +218,15 @@ def tile_picked_filmg_silu_e_kernel(tc, xT, w1, w2, w3, offs, cen, pos1, pos2, o
             nc.vector.tensor_tensor(total[:], acts[i][:, 0, :], acts[i][:, 1, :], ADD)
             nc.sync.dma_start(out[:, v0:v1], total[:])
 
+        centre(gc, g_sb, 0, PIECES[0])
+        centre(gc, g_sb, PIECES[0], V)
+        for a in range(2):
+            nc.scalar.copy(s_sb[:, half(a)], s_banks[a][:])
+        for v0, v1 in pieces:
+            centre(sc, s_sb, v0, v1)
         neighbours(0, PIECES[0])
         neighbours(PIECES[0], V)
-        shift(0)
-        shift(1)
-        shift(2)
+        for i in range(3):
+            shift(i)
         for i in range(3):
             finish(i)

@@ -173,10 +173,21 @@ def tile_picked_filmg_silu_e_kernel(tc, xT, w1, w2, w3, offs, cen, pos1, pos2, o
         g_banks = [ps.tile([P, HALF], F32, name="acc_g%d" % a) for a in range(2)]
         h_banks = [ps.tile([P, HALF], F32, name="acc_h%d" % a) for a in range(2)]
         s_banks = [ps.tile([P, HALF], F32, name="acc_s%d" % a) for a in range(2)]
-        for z in range(2):
-            for banks, both in ((g_banks, q1), (h_banks, q3)):
-                for a in range(2):
-                    one_pass(banks[a], a, both[z], z)
+        for a in range(2):
+            one_pass(g_banks[a], a, q1[0], 0)
+        unread = ps.tile([P, HALF], F32, name="unread")
+        nc.tensor.matmul_mx(
+            out=unread[:],
+            lhsT=q1[0][0].bitcast(FP8X4),
+            lhsT_scale=q1[0][1],
+            rhs=x_codes[0][:, half(0)].bitcast(FP8X4),
+            rhs_scale=x_scales[0][:, half(0)],
+            start=True,
+            stop=True,
+        )
+        for banks, both, z in ((h_banks, q3, 0), (g_banks, q1, 1), (h_banks, q3, 1)):
+            for a in range(2):
+                one_pass(banks[a], a, both[z], z)
 
         g_sb = results.tile([P, S], F32, name="res_g", offset=0, align_bytes=64)
         h_sb = sb.tile([P, S], F32, name="res_h", align_bytes=64)

@@ -107,16 +107,16 @@ def tile_picked_filmg_silu_e_kernel(tc, xT, w1, w2, w3, offs, cen, pos1, pos2, o
             nc.vector.quantize_mx(out=codes[:].bitcast(FP8X4), scales=scales[:], in_=rounded[:].rearrange("p n j -> p (n j)"))
             return [(codes[:, n0 : n0 + N], scales[:, n0 : n0 + N]) for n0 in range(0, width, N)]
 
-        def one_pass(bank, a, quantized_w, z):
+        def one_pass(bank, columns, quantized_w, z, start, stop):
             codes, scales = quantized_w
             nc.tensor.matmul_mx(
                 out=bank[:],
                 lhsT=codes.bitcast(FP8X4),
                 lhsT_scale=scales,
-                rhs=x_codes[z][:, half(a)].bitcast(FP8X4),
-                rhs_scale=x_scales[z][:, half(a)],
-                start=z == 0,
-                stop=z == 1,
+                rhs=x_codes[z][:, columns].bitcast(FP8X4),
+                rhs_scale=x_scales[z][:, columns],
+                start=start,
+                stop=stop,
             )
 
         for j in range(4):
@@ -170,34 +170,31 @@ def tile_picked_filmg_silu_e_kernel(tc, xT, w1, w2, w3, offs, cen, pos1, pos2, o
         q3 = q3 + quantize_w("w31", codes_tile("w31", 1), rounded31)
         round_w(nc.vector.tensor_copy, rounded2, 1, raw21)
 
-        g_banks = [ps.tile([P, HALF], F32, name="acc_g%d" % a) for a in range(2)]
+        g_parts = [half(0), quarter(2), quarter(3)]
+        g_banks = [ps.tile([P, part.stop - part.start], F32, name="acc_g%d" % part.start) for part in g_parts]
         h_banks = [ps.tile([P, HALF], F32, name="acc_h%d" % a) for a in range(2)]
         s_banks = [ps.tile([P, HALF], F32, name="acc_s%d" % a) for a in range(2)]
-        for a in range(2):
-            one_pass(g_banks[a], a, q1[0], 0)
+        for i in range(3):
+            one_pass(g_banks[i], g_parts[i], q1[0], 0, True, False)
         unread = ps.tile([P, HALF], F32, name="unread")
-        nc.tensor.matmul_mx(
-            out=unread[:],
-            lhsT=q1[0][0].bitcast(FP8X4),
-            lhsT_scale=q1[0][1],
-            rhs=x_codes[0][:, half(0)].bitcast(FP8X4),
-            rhs_scale=x_scales[0][:, half(0)],
-            start=True,
-            stop=True,
-        )
-        for banks, both, z in ((h_banks, q3, 0), (g_banks, q1, 1), (h_banks, q3, 1)):
-            for a in range(2):
-                one_pass(banks[a], a, both[z], z)
+        one_pass(unread, half(0), q1[0], 0, True, True)
+        for a in range(2):
+            one_pass(h_banks[a], half(a), q3[0], 0, True, False)
+        for i in range(3):
+            one_pass(g_banks[i], g_parts[i], q1[1], 1, False, True)
+        for a in range(2):
+            one_pass(h_banks[a], half(a), q3[1], 1, False, True)
 
         g_sb = results.tile([P, S], F32, name="res_g", offset=0, align_bytes=64)
         h_sb = sb.tile([P, S], F32, name="res_h", align_bytes=64)
         s_sb = sb.tile([P, S], F32, name="res_s", align_bytes=64)
-        nc.scalar.copy(g_sb[:, half(0)], g_banks[0][:])
-        nc.vector.tensor_copy(g_sb[:, half(1)], g_banks[1][:])
+        nc.scalar.copy(g_sb[:, g_parts[0]], g_banks[0][:])
+        for i in range(1, 3):
+            nc.vector.tensor_copy(g_sb[:, g_parts[i]], g_banks[i][:])
         q2 = quantize_w("w2", results.tile([P, 2 * N], U32, name="codes_w2", offset=4096, align_bytes=64), rounded2)
         for a in range(2):
             for z in range(2):
-                one_pass(s_banks[a], a, q2[z], z)
+                one_pass(s_banks[a], half(a), q2[z], z, z == 0, z == 1)
         nc.scalar.copy(h_sb[:, half(0)], h_banks[0][:])
         nc.vector.tensor_copy(h_sb[:, half(1)], h_banks[1][:])
 

@@ -125,8 +125,8 @@ def tile_picked_filmg_silu_e_kernel(tc, xT, w1, w2, w3, offs, cen, pos1, pos2, o
             weave_all(0, q)
             quantize_x(0, q - 1)
         quantize_x(0, 3)
-        for j in range(2):
-            gather_plane(load_plane(1, j), 1, j, 1, [(QUARTER, S)])
+        gather_plane(load_plane(1, 0), 1, 0, 1, [(QUARTER, S)])
+        gather_plane(load_plane(1, 1), 1, 1, 1, [(q * QUARTER, (q + 1) * QUARTER) for q in range(1, 4)])
         for q in range(1, 4):
             weave_two(nc.vector.tensor_copy, 1, q, 0)
         gather_plane(load_plane(1, 2), 1, 2, 2, [(HALF, S)])

@@ -52,7 +52,8 @@ def tile_picked_filmg_silu_e_kernel(tc, xT, w1, w2, w3, offs, cen, pos1, pos2, o
             return slice(a * HALF, (a + 1) * HALF)
 
         x_planes = xT.rearrange("(z p j) t -> z j p t", z=2, p=P, j=4)
-        woven = [[sb.tile([P, QUARTER, 4], BF16, name="woven%d%d" % (z, q), align_bytes=64) for q in range(4)] for z in range(2)]
+        woven = [[sb.tile([P, QUARTER, 4], BF16, name="woven%d%d" % (z, q), align_bytes=64) for q in range(4 - z)] for z in range(2)]
+        woven[1].append(results.tile([P, QUARTER, 4], BF16, name="woven13", offset=5120, align_bytes=64))
         picked = [sb.tile([P, 4, S], BF16, name="picked%d" % z, align_bytes=64) for z in range(2)]
         x_codes = [sb.tile([P, S], U32, name="x_codes0", align_bytes=64)]
         x_scales = [sb.tile([P, S], U8, name="x_scales%d" % z, align_bytes=64) for z in range(2)]
@@ -152,12 +153,12 @@ def tile_picked_filmg_silu_e_kernel(tc, xT, w1, w2, w3, offs, cen, pos1, pos2, o
         rounded11 = rounded_tile("w11", 1)
         rounded30 = rounded_tile("w30", 1)
         rounded31 = rounded_tile("w31", 1)
-        rounded2 = rounded_tile("w2", 2)
+        rounded20 = rounded_tile("w20", 1)
+        rounded21 = rounded_tile("w21", 1)
         nc.gpsimd.tensor_scalar(rounded30[:], raw30[:].rearrange("p j n -> p n j"), 1.0, 0.0, MULT, ADD)
         weave_two(nc.scalar.copy, 1, 2, 2)
         weave_two(nc.scalar.copy, 1, 3, 2)
-        round_w(nc.scalar.copy, rounded31, 0, raw31)
-        round_w(nc.scalar.copy, rounded2, 0, raw20)
+        round_w(nc.scalar.copy, rounded20, 0, raw20)
 
         q3 = quantize_w("w30", codes_tile("w30", 1), rounded30)
         x_codes.append(shared.tile([P, S], U32, name="x_codes1", offset=0, align_bytes=64))
@@ -165,36 +166,41 @@ def tile_picked_filmg_silu_e_kernel(tc, xT, w1, w2, w3, offs, cen, pos1, pos2, o
         round_w(nc.vector.tensor_copy, rounded11, 0, raw11)
         quantize_x(1, 1)
         q1 = q1 + quantize_w("w11", results.tile([P, N], U32, name="codes_w11", offset=4096, align_bytes=64), rounded11)
+        round_w(nc.vector.tensor_copy, rounded31, 0, raw31)
         quantize_x(1, 2)
-        quantize_x(1, 3)
         q3 = q3 + quantize_w("w31", codes_tile("w31", 1), rounded31)
-        round_w(nc.vector.tensor_copy, rounded2, 1, raw21)
+        quantize_x(1, 3)
+        round_w(nc.vector.tensor_copy, rounded21, 0, raw21)
+        q2 = quantize_w("w20", results.tile([P, N], U32, name="codes_w20", offset=5120, align_bytes=64), rounded20)
 
         g_parts = [half(0), quarter(2), quarter(3)]
         g_banks = [ps.tile([P, part.stop - part.start], F32, name="acc_g%d" % part.start) for part in g_parts]
         h_banks = [ps.tile([P, HALF], F32, name="acc_h%d" % a) for a in range(2)]
-        s_banks = [ps.tile([P, HALF], F32, name="acc_s%d" % a) for a in range(2)]
         for i in range(3):
             one_pass(g_banks[i], g_parts[i], q1[0], 0, True, False)
-        unread = ps.tile([P, HALF], F32, name="unread")
+        unread = ps.tile([P, HALF], F32, name="unread", tag="spare")
         one_pass(unread, half(0), q1[0], 0, True, True)
         for a in range(2):
             one_pass(h_banks[a], half(a), q3[0], 0, True, False)
-        for i in range(3):
+        for i in range(2):
             one_pass(g_banks[i], g_parts[i], q1[1], 1, False, True)
-        for a in range(2):
-            one_pass(h_banks[a], half(a), q3[1], 1, False, True)
+        one_pass(h_banks[0], half(0), q3[1], 1, False, True)
+        one_pass(g_banks[2], g_parts[2], q1[1], 1, False, True)
+        one_pass(h_banks[1], half(1), q3[1], 1, False, True)
 
         g_sb = results.tile([P, S], F32, name="res_g", offset=0, align_bytes=64)
         h_sb = sb.tile([P, S], F32, name="res_h", align_bytes=64)
         s_sb = sb.tile([P, S], F32, name="res_s", align_bytes=64)
-        nc.scalar.copy(g_sb[:, g_parts[0]], g_banks[0][:])
-        for i in range(1, 3):
-            nc.vector.tensor_copy(g_sb[:, g_parts[i]], g_banks[i][:])
-        q2 = quantize_w("w2", results.tile([P, 2 * N], U32, name="codes_w2", offset=4096, align_bytes=64), rounded2)
-        for a in range(2):
-            for z in range(2):
-                one_pass(s_banks[a], half(a), q2[z], z, z == 0, z == 1)
+        for i in range(2):
+            nc.scalar.copy(g_sb[:, g_parts[i]], g_banks[i][:])
+        nc.vector.tensor_copy(g_sb[:, g_parts[2]], g_banks[2][:])
+        q2 = q2 + quantize_w("w21", results.tile([P, N], U32, name="codes_w21", offset=4096, align_bytes=64), rounded21)
+        s_parts = [quarter(0), quarter(1), half(1)]
+        s_banks = [ps.tile([P, QUARTER], F32, name="acc_s0", tag="spare")]
+        s_banks.extend(ps.tile([P, part.stop - part.start], F32, name="acc_s%d" % part.start) for part in s_parts[1:])
+        for z in range(2):
+            for i in range(3):
+                one_pass(s_banks[i], s_parts[i], q2[z], z, z == 0, z == 1)
         nc.scalar.copy(h_sb[:, half(0)], h_banks[0][:])
         nc.vector.tensor_copy(h_sb[:, half(1)], h_banks[1][:])
 
@@ -228,8 +234,9 @@ def tile_picked_filmg_silu_e_kernel(tc, xT, w1, w2, w3, offs, cen, pos1, pos2, o
 
         centre(gc, g_sb, 0, PIECES[0])
         centre(gc, g_sb, PIECES[0], V)
-        for a in range(2):
-            nc.scalar.copy(s_sb[:, half(a)], s_banks[a][:])
+        nc.vector.tensor_copy(s_sb[:, s_parts[0]], s_banks[0][:])
+        for i in range(1, 3):
+            nc.scalar.copy(s_sb[:, s_parts[i]], s_banks[i][:])
         for v0, v1 in pieces:
             centre(sc, s_sb, v0, v1)
         neighbours(0, PIECES[0])

@@ -21,7 +21,6 @@ PER_COLUMN = 16
 HALF = S // 2
 QUARTER = S // 4
 PIECES = [192, 192, 128]
-HEAD = 1152
 
 
 def tile_picked_filmg_silu_e_kernel(tc, xT, w1, w2, w3, offs, cen, pos1, pos2, out):
@@ -54,7 +53,6 @@ def tile_picked_filmg_silu_e_kernel(tc, xT, w1, w2, w3, offs, cen, pos1, pos2, o
         x_planes = xT.rearrange("(z p j) t -> z j p t", z=2, p=P, j=4)
         woven = [[sb.tile([P, QUARTER, 4], BF16, name="woven%d%d" % (z, q), align_bytes=64) for q in range(4 - z)] for z in range(2)]
         woven[1].append(results.tile([P, QUARTER, 4], BF16, name="woven13", offset=5120, align_bytes=64))
-        picked = [sb.tile([P, 4, S], BF16, name="picked%d" % z, align_bytes=64) for z in range(2)]
         x_codes = [sb.tile([P, S], U32, name="x_codes0", align_bytes=64)]
         x_scales = [sb.tile([P, S], U8, name="x_scales%d" % z, align_bytes=64) for z in range(2)]
 
@@ -68,20 +66,11 @@ def tile_picked_filmg_silu_e_kernel(tc, xT, w1, w2, w3, offs, cen, pos1, pos2, o
                 nc.sync.dma_start(offs_sb[:], offs)
             return plane
 
-        def gather_plane(plane, z, j, on_vector, cuts):
-            for q in range(on_vector):
+        def gather_plane(plane, z, j):
+            for q in range(2):
                 nc.vector.tensor_copy(woven[z][q][:, :, j], plane[:].indirect(entries(offs_sb, q * QUARTER, (q + 1) * QUARTER)))
-            for n0, n1 in cuts:
-                nc.scalar.activation(picked[z][:, j, n0:n1], plane[:].indirect(entries(offs_sb, n0, n1)), COPY)
-
-        def weave_all(z, q):
-            nc.vector.tensor_copy(
-                woven[z][q][:].rearrange("p (c i) j -> p c j i", i=4),
-                picked[z][:, :, quarter(q)].rearrange("p j (c i) -> p c j i", i=4),
-            )
-
-        def weave_two(copy, z, q, j0):
-            copy(woven[z][q][:, :, j0 : j0 + 2], picked[z][:, j0 : j0 + 2, quarter(q)].rearrange("p j n -> p n j"))
+            for q in range(2, 4):
+                nc.scalar.activation(woven[z][q][:, :, j], plane[:].indirect(entries(offs_sb, q * QUARTER, (q + 1) * QUARTER)), COPY)
 
         def quantize_x(z, q):
             nc.vector.quantize_mx(out=x_codes[z][:, quarter(q)].bitcast(FP8X4), scales=x_scales[z][:, quarter(q)], in_=woven[z][q][:].rearrange("p n j -> p (n j)"))
@@ -121,25 +110,18 @@ def tile_picked_filmg_silu_e_kernel(tc, xT, w1, w2, w3, offs, cen, pos1, pos2, o
             )
 
         for j in range(4):
-            gather_plane(load_plane(0, j), 0, j, 1, [(QUARTER, S)])
-        for q in range(1, 4):
-            weave_all(0, q)
-            quantize_x(0, q - 1)
-        quantize_x(0, 3)
-        gather_plane(load_plane(1, 0), 1, 0, 1, [(QUARTER, S)])
-        gather_plane(load_plane(1, 1), 1, 1, 1, [(q * QUARTER, (q + 1) * QUARTER) for q in range(1, 4)])
-        for q in range(1, 4):
-            weave_two(nc.vector.tensor_copy, 1, q, 0)
-        gather_plane(load_plane(1, 2), 1, 2, 2, [(HALF, S)])
+            gather_plane(load_plane(0, j), 0, j)
+        for q in range(4):
+            quantize_x(0, q)
+        for j in range(3):
+            gather_plane(load_plane(1, j), 1, j)
 
-        last = plane_tile(1, 3)
-        nc.sync.dma_start(last[:, :HEAD], x_planes[1, 3][:, :HEAD])
         raw10 = load_w(raw_tile("w10"), w1, 0)
-        nc.sync.dma_start(last[:, HEAD:], x_planes[1, 3][:, HEAD:])
+        last = load_plane(1, 3)
         rounded10 = rounded_tile("w10", 1)
-        round_w(nc.scalar.copy, rounded10, 0, raw10)
+        round_w(nc.vector.tensor_copy, rounded10, 0, raw10)
         q1 = quantize_w("w10", codes_tile("w10", 1), rounded10)
-        gather_plane(last, 1, 3, 2, [(HALF, 3 * QUARTER), (3 * QUARTER, S)])
+        gather_plane(last, 1, 3)
 
         raw30 = load_w(shared.tile([P, 4, N], F32, name="raw_w30", offset=3584, align_bytes=64), w3, 0)
         raw11 = load_w(raw_tile("w11"), w1, 1)
@@ -156,8 +138,7 @@ def tile_picked_filmg_silu_e_kernel(tc, xT, w1, w2, w3, offs, cen, pos1, pos2, o
         rounded20 = rounded_tile("w20", 1)
         rounded21 = rounded_tile("w21", 1)
         nc.gpsimd.tensor_scalar(rounded30[:], raw30[:].rearrange("p j n -> p n j"), 1.0, 0.0, MULT, ADD)
-        weave_two(nc.scalar.copy, 1, 2, 2)
-        weave_two(nc.scalar.copy, 1, 3, 2)
+        round_w(nc.scalar.copy, rounded31, 0, raw31)
         round_w(nc.scalar.copy, rounded20, 0, raw20)
 
         q3 = quantize_w("w30", codes_tile("w30", 1), rounded30)
@@ -166,7 +147,6 @@ def tile_picked_filmg_silu_e_kernel(tc, xT, w1, w2, w3, offs, cen, pos1, pos2, o
         round_w(nc.vector.tensor_copy, rounded11, 0, raw11)
         quantize_x(1, 1)
         q1 = q1 + quantize_w("w11", results.tile([P, N], U32, name="codes_w11", offset=4096, align_bytes=64), rounded11)
-        round_w(nc.vector.tensor_copy, rounded31, 0, raw31)
         quantize_x(1, 2)
         q3 = q3 + quantize_w("w31", codes_tile("w31", 1), rounded31)
         quantize_x(1, 3)

@@ -21,6 +21,7 @@ PER_COLUMN = 16
 HALF = S // 2
 QUARTER = S // 4
 PIECES = [192, 192, 128]
+LIGHT_SHARE = 384
 
 
 def tile_picked_filmg_silu_e_kernel(tc, xT, w1, w2, w3, offs, cen, pos1, pos2, out):
@@ -51,8 +52,10 @@ def tile_picked_filmg_silu_e_kernel(tc, xT, w1, w2, w3, offs, cen, pos1, pos2, o
             return slice(a * HALF, (a + 1) * HALF)
 
         x_planes = xT.rearrange("(z p j) t -> z j p t", z=2, p=P, j=4)
-        woven = [[sb.tile([P, QUARTER, 4], BF16, name="woven%d%d" % (z, q), align_bytes=64) for q in range(4 - z)] for z in range(2)]
-        woven[1].append(results.tile([P, QUARTER, 4], BF16, name="woven13", offset=5120, align_bytes=64))
+        woven = [
+            sb.tile([P, 4 * S], BF16, name="woven0", align_bytes=64),
+            results.tile([P, 4 * S], BF16, name="woven1", offset=5120, align_bytes=64),
+        ]
         x_codes = [sb.tile([P, S], U32, name="x_codes0", align_bytes=64)]
         x_scales = [sb.tile([P, S], U8, name="x_scales%d" % z, align_bytes=64) for z in range(2)]
 
@@ -66,14 +69,14 @@ def tile_picked_filmg_silu_e_kernel(tc, xT, w1, w2, w3, offs, cen, pos1, pos2, o
                 nc.sync.dma_start(offs_sb[:], offs)
             return plane
 
-        def gather_plane(plane, z, j):
-            for q in range(2):
-                nc.vector.tensor_copy(woven[z][q][:, :, j], plane[:].indirect(entries(offs_sb, q * QUARTER, (q + 1) * QUARTER)))
-            for q in range(2, 4):
-                nc.scalar.activation(woven[z][q][:, :, j], plane[:].indirect(entries(offs_sb, q * QUARTER, (q + 1) * QUARTER)), COPY)
+        def gather_plane(plane, z, j, vector_cuts, scalar_cuts):
+            for n0, n1 in zip(vector_cuts[:-1], vector_cuts[1:]):
+                nc.vector.tensor_copy(woven[z][:, 4 * n0 + j : 4 * n1 : 4], plane[:].indirect(entries(offs_sb, n0, n1)))
+            for n0, n1 in zip(scalar_cuts[:-1], scalar_cuts[1:]):
+                nc.scalar.activation(woven[z][:, 4 * n0 + j : 4 * n1 : 4], plane[:].indirect(entries(offs_sb, n0, n1)), COPY)
 
         def quantize_x(z, q):
-            nc.vector.quantize_mx(out=x_codes[z][:, quarter(q)].bitcast(FP8X4), scales=x_scales[z][:, quarter(q)], in_=woven[z][q][:].rearrange("p n j -> p (n j)"))
+            nc.vector.quantize_mx(out=x_codes[z][:, quarter(q)].bitcast(FP8X4), scales=x_scales[z][:, quarter(q)], in_=woven[z][:, 4 * q * QUARTER : 4 * (q + 1) * QUARTER])
 
         def load_w(raw, w, z):
             nc.sync.dma_start(raw[:], w.rearrange("(z p j) n -> z p j n", z=2, p=P, j=4)[z])
@@ -110,18 +113,19 @@ def tile_picked_filmg_silu_e_kernel(tc, xT, w1, w2, w3, offs, cen, pos1, pos2, o
             )
 
         for j in range(4):
-            gather_plane(load_plane(0, j), 0, j)
+            gather_plane(load_plane(0, j), 0, j, [0, HALF], [HALF, S])
         for q in range(4):
             quantize_x(0, q)
-        for j in range(3):
-            gather_plane(load_plane(1, j), 1, j)
+        for j in range(2):
+            gather_plane(load_plane(1, j), 1, j, [0, LIGHT_SHARE], [LIGHT_SHARE, S])
+        gather_plane(load_plane(1, 2), 1, 2, [0, HALF], [HALF, S])
 
         raw10 = load_w(raw_tile("w10"), w1, 0)
         last = load_plane(1, 3)
         rounded10 = rounded_tile("w10", 1)
         round_w(nc.vector.tensor_copy, rounded10, 0, raw10)
         q1 = quantize_w("w10", codes_tile("w10", 1), rounded10)
-        gather_plane(last, 1, 3)
+        gather_plane(last, 1, 3, [0, QUARTER, HALF], [HALF, 3 * QUARTER, S])
 
         raw30 = load_w(shared.tile([P, 4, N], F32, name="raw_w30", offset=3584, align_bytes=64), w3, 0)
         raw11 = load_w(raw_tile("w11"), w1, 1)

@@ -118,14 +118,14 @@ def tile_picked_filmg_silu_e_kernel(tc, xT, w1, w2, w3, offs, cen, pos1, pos2, o
             quantize_x(0, q)
         for j in range(2):
             gather_plane(load_plane(1, j), 1, j, [0, LIGHT_SHARE], [LIGHT_SHARE, S])
-        gather_plane(load_plane(1, 2), 1, 2, [0, HALF], [HALF, S])
+        gather_plane(load_plane(1, 2), 1, 2, [0, LIGHT_SHARE], [LIGHT_SHARE, S])
 
         raw10 = load_w(raw_tile("w10"), w1, 0)
         last = load_plane(1, 3)
         rounded10 = rounded_tile("w10", 1)
         round_w(nc.vector.tensor_copy, rounded10, 0, raw10)
         q1 = quantize_w("w10", codes_tile("w10", 1), rounded10)
-        gather_plane(last, 1, 3, [0, QUARTER, HALF], [HALF, 3 * QUARTER, S])
+        gather_plane(last, 1, 3, [0, LIGHT_SHARE], [LIGHT_SHARE, HALF, 3 * QUARTER, S])
 
         raw30 = load_w(shared.tile([P, 4, N], F32, name="raw_w30", offset=3584, align_bytes=64), w3, 0)
         raw11 = load_w(raw_tile("w11"), w1, 1)

@@ -20,7 +20,7 @@ P = 128
 PER_COLUMN = 16
 HALF = S // 2
 QUARTER = S // 4
-PIECES = [192, 192, 128]
+PIECES = [128, 128, 128, 128]
 LIGHT_SHARE = 384
 
 
@@ -190,17 +190,19 @@ def tile_picked_filmg_silu_e_kernel(tc, xT, w1, w2, w3, offs, cen, pos1, pos2, o
 
         bounds = [sum(PIECES[:i]) for i in range(len(PIECES) + 1)]
         pieces = list(zip(bounds[:-1], bounds[1:]))
-        gc = sb.tile([P, V], F32, name="gc")
+        product_cuts = [(0, 128), (128, 384), (384, V)]
+        gc = [sb.tile([P, v1 - v0], F32, name="gc%d" % v0) for v0, v1 in product_cuts[:-1]]
         sc = sb.tile([P, V], F32, name="sc")
         prod = sb.tile([P, 2, V], F32, name="prod")
         acts = []
 
         def centre(dst, src, v0, v1):
-            nc.scalar.activation(dst[:, v0:v1], src[:].indirect(entries(cen_sb, v0, v1)), COPY)
+            nc.scalar.activation(dst, src[:].indirect(entries(cen_sb, v0, v1)), COPY)
 
-        def neighbours(v0, v1):
+        def neighbours(i):
+            v0, v1 = product_cuts[i]
             for d in range(2):
-                nc.vector.tensor_tensor(prod[:, d, v0:v1], h_sb[:].indirect(entries(pos_sb[d], v0, v1)), gc[:, v0:v1], MULT)
+                nc.vector.tensor_tensor(prod[:, d, v0:v1], h_sb[:].indirect(entries(pos_sb[d], v0, v1)), gc[i][:], MULT)
 
         def shift(i):
             v0, v1 = pieces[i]
@@ -216,16 +218,18 @@ def tile_picked_filmg_silu_e_kernel(tc, xT, w1, w2, w3, offs, cen, pos1, pos2, o
             nc.vector.tensor_tensor(total[:], acts[i][:, 0, :], acts[i][:, 1, :], ADD)
             nc.sync.dma_start(out[:, v0:v1], total[:])
 
-        centre(gc, g_sb, 0, PIECES[0])
-        centre(gc, g_sb, PIECES[0], V)
+        for i in range(2):
+            centre(gc[i][:], g_sb, *product_cuts[i])
         nc.vector.tensor_copy(s_sb[:, s_parts[0]], s_banks[0][:])
         for i in range(1, 3):
             nc.scalar.copy(s_sb[:, s_parts[i]], s_banks[i][:])
-        for v0, v1 in pieces:
-            centre(sc, s_sb, v0, v1)
-        neighbours(0, PIECES[0])
-        neighbours(PIECES[0], V)
+        gc.append(results.tile([P, 128], F32, name="gc_last", offset=4096, align_bytes=64))
+        centre(gc[2][:], g_sb, *product_cuts[2])
+        for v0 in (0, V // 2):
+            centre(sc[:, v0 : v0 + V // 2], s_sb, v0, v0 + V // 2)
         for i in range(3):
+            neighbours(i)
+        for i in range(len(PIECES)):
             shift(i)
-        for i in range(3):
+        for i in range(len(PIECES)):
             finish(i)

@@ -141,7 +141,7 @@ def tile_picked_filmg_silu_e_kernel(tc, xT, w1, w2, w3, offs, cen, pos1, pos2, o
         rounded31 = rounded_tile("w31", 1)
         rounded20 = rounded_tile("w20", 1)
         rounded21 = rounded_tile("w21", 1)
-        nc.gpsimd.tensor_scalar(rounded30[:], raw30[:].rearrange("p j n -> p n j"), 1.0, 0.0, MULT, ADD)
+        nc.gpsimd.tensor_scalar(rounded30[:].rearrange("p (c i) j -> p c j i", i=4), raw30[:].rearrange("p j (c i) -> p c j i", i=4), 1.0, 0.0, MULT, ADD)
         round_w(nc.scalar.copy, rounded31, 0, raw31)
         round_w(nc.scalar.copy, rounded20, 0, raw20)
 

from contextlib import ExitStack

import concourse.mybir as mybir

K, T, S, V, N = 1024, 2048, 1024, 512, 128
FLOPS = 3 * 2 * K * S * N

F32 = mybir.dt.float32
BF16 = mybir.dt.bfloat16
U32 = mybir.dt.uint32
U16 = mybir.dt.uint16
U8 = mybir.dt.uint8
FP8X4 = mybir.dt.float8_e4m3fn_x4
MULT = mybir.AluOpType.mult
ADD = mybir.AluOpType.add
SILU = mybir.ActivationFunctionType.Silu
COPY = mybir.ActivationFunctionType.Copy

P = 128
PER_COLUMN = 16
HALF = S // 2
QUARTER = S // 4
PIECES = [128, 128, 128, 128]
LIGHT_SHARE = 384


def tile_picked_filmg_silu_e_kernel(tc, xT, w1, w2, w3, offs, cen, pos1, pos2, out):
    nc = tc.nc
    with ExitStack() as ctx:
        lists = ctx.enter_context(tc.tile_pool(name="lists", bufs=1))
        sb = ctx.enter_context(tc.tile_pool(name="sb", bufs=1))
        shared = ctx.enter_context(tc.tile_pool(name="shared", bufs=1))
        results = ctx.enter_context(tc.tile_pool(name="results", bufs=1))
        ps = ctx.enter_context(tc.psum_pool(name="ps", bufs=1))

        offs_sb = lists.tile([P, S // PER_COLUMN], U16, name="offs_sb")
        cen_sb = lists.tile([P, V // PER_COLUMN], U16, name="cen_sb")
        pos_sb = [lists.tile([P, V // PER_COLUMN], U16, name="pos%d_sb" % d) for d in range(2)]

        zero_in = sb.tile([P, 1], F32, name="zero_in")
        zero = sb.tile([P, 1], F32, name="zero")
        nc.gpsimd.memset(zero_in[:], 0.0)
        nc.scalar.activation(zero[:], zero_in[:], SILU)

        def entries(tile, n0, n1):
            return tile[:, n0 // PER_COLUMN : n1 // PER_COLUMN]

        def quarter(q):
            return slice(q * QUARTER, (q + 1) * QUARTER)

        def half(a):
            return slice(a * HALF, (a + 1) * HALF)

        x_planes = xT.rearrange("(z p j) t -> z j p t", z=2, p=P, j=4)
        woven = [
            sb.tile([P, 4 * S], BF16, name="woven0", align_bytes=64),
            results.tile([P, 4 * S], BF16, name="woven1", offset=5120, align_bytes=64),
        ]
        x_codes = [sb.tile([P, S], U32, name="x_codes0", align_bytes=64)]
        x_scales = [sb.tile([P, S], U8, name="x_scales%d" % z, align_bytes=64) for z in range(2)]

        def plane_tile(z, j):
            return sb.tile([P, T], F32, name="plane%d%d" % (z, j), align_bytes=64)

        def load_plane(z, j):
            plane = plane_tile(z, j)
            nc.sync.dma_start(plane[:], x_planes[z, j])
            if (z, j) == (0, 0):
                nc.sync.dma_start(offs_sb[:], offs)
            return plane

        def gather_plane(plane, z, j, vector_cuts, scalar_cuts):
            for n0, n1 in zip(vector_cuts[:-1], vector_cuts[1:]):
                nc.vector.tensor_copy(woven[z][:, 4 * n0 + j : 4 * n1 : 4], plane[:].indirect(entries(offs_sb, n0, n1)))
            for n0, n1 in zip(scalar_cuts[:-1], scalar_cuts[1:]):
                nc.scalar.activation(woven[z][:, 4 * n0 + j : 4 * n1 : 4], plane[:].indirect(entries(offs_sb, n0, n1)), COPY)

        def quantize_x(z, q):
            nc.vector.quantize_mx(out=x_codes[z][:, quarter(q)].bitcast(FP8X4), scales=x_scales[z][:, quarter(q)], in_=woven[z][:, 4 * q * QUARTER : 4 * (q + 1) * QUARTER])

        def load_w(raw, w, z):
            nc.sync.dma_start(raw[:], w.rearrange("(z p j) n -> z p j n", z=2, p=P, j=4)[z])
            return raw

        def raw_tile(name):
            return sb.tile([P, 4, N], F32, name="raw_" + name, align_bytes=64)

        def rounded_tile(name, passes):
            return sb.tile([P, passes * N, 4], BF16, name="rounded_" + name, align_bytes=64)

        def round_w(copy, rounded, at, raw):
            copy(rounded[:, at * N : (at + 1) * N].rearrange("p (c i) j -> p c j i", i=4), raw[:].rearrange("p j (c i) -> p c j i", i=4))

        def codes_tile(name, passes):
            return sb.tile([P, passes * N], U32, name="codes_" + name, align_bytes=64)

        def quantize_w(name, codes, rounded):
            width = rounded.shape[1]
            scales = sb.tile([P, width], U8, name="scales_" + name, align_bytes=64)
            nc.vector.quantize_mx(out=codes[:].bitcast(FP8X4), scales=scales[:], in_=rounded[:].rearrange("p n j -> p (n j)"))
            return [(codes[:, n0 : n0 + N], scales[:, n0 : n0 + N]) for n0 in range(0, width, N)]

        def one_pass(bank, columns, quantized_w, z, start, stop):
            codes, scales = quantized_w
            nc.tensor.matmul_mx(
                out=bank[:],
                lhsT=codes.bitcast(FP8X4),
                lhsT_scale=scales,
                rhs=x_codes[z][:, columns].bitcast(FP8X4),
                rhs_scale=x_scales[z][:, columns],
                start=start,
                stop=stop,
            )

        for j in range(4):
            gather_plane(load_plane(0, j), 0, j, [0, HALF], [HALF, S])
        for q in range(4):
            quantize_x(0, q)
        for j in range(2):
            gather_plane(load_plane(1, j), 1, j, [0, LIGHT_SHARE], [LIGHT_SHARE, S])
        gather_plane(load_plane(1, 2), 1, 2, [0, LIGHT_SHARE], [LIGHT_SHARE, S])

        raw10 = load_w(raw_tile("w10"), w1, 0)
        last = load_plane(1, 3)
        rounded10 = rounded_tile("w10", 1)
        round_w(nc.vector.tensor_copy, rounded10, 0, raw10)
        q1 = quantize_w("w10", codes_tile("w10", 1), rounded10)
        gather_plane(last, 1, 3, [0, LIGHT_SHARE], [LIGHT_SHARE, HALF, 3 * QUARTER, S])

        raw30 = load_w(shared.tile([P, 4, N], F32, name="raw_w30", offset=3584, align_bytes=64), w3, 0)
        raw11 = load_w(raw_tile("w11"), w1, 1)
        raw31 = load_w(raw_tile("w31"), w3, 1)
        raw20 = load_w(results.tile([P, 4, N], F32, name="raw_w20", offset=0, align_bytes=64), w2, 0)
        raw21 = load_w(raw_tile("w21"), w2, 1)
        nc.sync.dma_start(cen_sb[:], cen)
        nc.sync.dma_start(pos_sb[0][:], pos1)
        nc.sync.dma_start(pos_sb[1][:], pos2)

        rounded11 = rounded_tile("w11", 1)
        rounded30 = rounded_tile("w30", 1)
        rounded31 = rounded_tile("w31", 1)
        rounded20 = rounded_tile("w20", 1)
        rounded21 = rounded_tile("w21", 1)
        nc.gpsimd.tensor_scalar(rounded30[:].rearrange("p (c i) j -> p c j i", i=4), raw30[:].rearrange("p j (c i) -> p c j i", i=4), 1.0, 0.0, MULT, ADD)
        round_w(nc.scalar.copy, rounded31, 0, raw31)
        round_w(nc.scalar.copy, rounded20, 0, raw20)

        q3 = quantize_w("w30", codes_tile("w30", 1), rounded30)
        x_codes.append(shared.tile([P, S], U32, name="x_codes1", offset=0, align_bytes=64))
        quantize_x(1, 0)
        round_w(nc.vector.tensor_copy, rounded11, 0, raw11)
        quantize_x(1, 1)
        q1 = q1 + quantize_w("w11", results.tile([P, N], U32, name="codes_w11", offset=4096, align_bytes=64), rounded11)
        quantize_x(1, 2)
        q3 = q3 + quantize_w("w31", codes_tile("w31", 1), rounded31)
        quantize_x(1, 3)
        round_w(nc.vector.tensor_copy, rounded21, 0, raw21)
        q2 = quantize_w("w20", results.tile([P, N], U32, name="codes_w20", offset=5120, align_bytes=64), rounded20)

        g_parts = [half(0), quarter(2), quarter(3)]
        g_banks = [ps.tile([P, part.stop - part.start], F32, name="acc_g%d" % part.start) for part in g_parts]
        h_banks = [ps.tile([P, HALF], F32, name="acc_h%d" % a) for a in range(2)]
        for i in range(3):
            one_pass(g_banks[i], g_parts[i], q1[0], 0, True, False)
        unread = ps.tile([P, HALF], F32, name="unread", tag="spare")
        one_pass(unread, half(0), q1[0], 0, True, True)
        for a in range(2):
            one_pass(h_banks[a], half(a), q3[0], 0, True, False)
        for i in range(2):
            one_pass(g_banks[i], g_parts[i], q1[1], 1, False, True)
        one_pass(h_banks[0], half(0), q3[1], 1, False, True)
        one_pass(g_banks[2], g_parts[2], q1[1], 1, False, True)
        one_pass(h_banks[1], half(1), q3[1], 1, False, True)

        g_sb = results.tile([P, S], F32, name="res_g", offset=0, align_bytes=64)
        h_sb = sb.tile([P, S], F32, name="res_h", align_bytes=64)
        s_sb = sb.tile([P, S], F32, name="res_s", align_bytes=64)
        for i in range(2):
            nc.scalar.copy(g_sb[:, g_parts[i]], g_banks[i][:])
        nc.vector.tensor_copy(g_sb[:, g_parts[2]], g_banks[2][:])
        q2 = q2 + quantize_w("w21", results.tile([P, N], U32, name="codes_w21", offset=4096, align_bytes=64), rounded21)
        s_parts = [quarter(0), quarter(1), half(1)]
        s_banks = [ps.tile([P, QUARTER], F32, name="acc_s0", tag="spare")]
        s_banks.extend(ps.tile([P, part.stop - part.start], F32, name="acc_s%d" % part.start) for part in s_parts[1:])
        for z in range(2):
            for i in range(3):
                one_pass(s_banks[i], s_parts[i], q2[z], z, z == 0, z == 1)
        nc.scalar.copy(h_sb[:, half(0)], h_banks[0][:])
        nc.vector.tensor_copy(h_sb[:, half(1)], h_banks[1][:])

        bounds = [sum(PIECES[:i]) for i in range(len(PIECES) + 1)]
        pieces = list(zip(bounds[:-1], bounds[1:]))
        product_cuts = [(0, 128), (128, 384), (384, V)]
        gc = [sb.tile([P, v1 - v0], F32, name="gc%d" % v0) for v0, v1 in product_cuts[:-1]]
        sc = sb.tile([P, V], F32, name="sc")
        prod = sb.tile([P, 2, V], F32, name="prod")
        acts = []

        def centre(dst, src, v0, v1):
            nc.scalar.activation(dst, src[:].indirect(entries(cen_sb, v0, v1)), COPY)

        def neighbours(i):
            v0, v1 = product_cuts[i]
            for d in range(2):
                nc.vector.tensor_tensor(prod[:, d, v0:v1], h_sb[:].indirect(entries(pos_sb[d], v0, v1)), gc[i][:], MULT)

        def shift(i):
            v0, v1 = pieces[i]
            pre = sb.tile([P, 2, v1 - v0], F32, name="pre%d" % i)
            act = sb.tile([P, 2, v1 - v0], F32, name="act%d" % i)
            nc.vector.tensor_tensor(pre[:], prod[:, :, v0:v1], sc[:, v0:v1].unsqueeze(1).to_broadcast([P, 2, v1 - v0]), ADD)
            nc.scalar.activation(act[:], pre[:], SILU, bias=zero[:])
            acts.append(act)

        def finish(i):
            v0, v1 = pieces[i]
            total = sb.tile([P, v1 - v0], F32, name="total%d" % i)
            nc.vector.tensor_tensor(total[:], acts[i][:, 0, :], acts[i][:, 1, :], ADD)
            nc.sync.dma_start(out[:, v0:v1], total[:])

        for i in range(2):
            centre(gc[i][:], g_sb, *product_cuts[i])
        nc.vector.tensor_copy(s_sb[:, s_parts[0]], s_banks[0][:])
        for i in range(1, 3):
            nc.scalar.copy(s_sb[:, s_parts[i]], s_banks[i][:])
        gc.append(results.tile([P, 128], F32, name="gc_last", offset=4096, align_bytes=64))
        centre(gc[2][:], g_sb, *product_cuts[2])
        for v0 in (0, V // 2):
            centre(sc[:, v0 : v0 + V // 2], s_sb, v0, v0 + V // 2)
        for i in range(3):
            neighbours(i)
        for i in range(len(PIECES)):
            shift(i)
        for i in range(len(PIECES)):
            finish(i)
